import numpy as np
import ml_dtypes


def mxq(x, axis, fmt="e4m3"):
    dtype, down = {"e4m3": (ml_dtypes.float8_e4m3fn, 7), "e5m2": (ml_dtypes.float8_e5m2, 14)}[fmt]
    v = np.moveaxis(np.asarray(x, np.float32).astype(ml_dtypes.bfloat16).astype(np.float64), axis, -1)
    blocks = v.reshape(v.shape[:-1] + (-1, 32))
    amax = np.abs(blocks).max(-1, keepdims=True)
    byte = np.maximum(np.where(amax > 0, np.frexp(amax)[1] - 1 + 127, 0) - down, 1)
    scale = np.exp2(byte - 127.0)
    codes = (blocks / scale).astype(np.float32).astype(dtype).astype(np.float64)
    return np.moveaxis((codes * scale).reshape(v.shape), -1, axis)


WIDE = False


def mx_kscale(k):
    if not WIDE:
        return np.ones(k)
    levels = np.array([10, -10, 5, -5, 0])
    if k % 512:
        return np.exp2(np.random.permutation(np.resize(levels, k // 32))).repeat(32)
    a = np.empty((k // 512, 16))
    for p in range(k // 512):
        a[p, :8] = np.random.permutation(np.resize(levels, 8))
        for g in range(8):
            far = levels[np.abs(levels - a[p, g]) >= 10]
            a[p, g + 8] = far[np.random.randint(len(far))]
    return np.exp2(a.ravel()).repeat(32)


BF16 = ml_dtypes.bfloat16


def bf(x):
    return np.asarray(x, np.float32).astype(BF16)


def f64(x):
    return np.asarray(x).astype(np.float64)

def planes(Y):
    n, m = Y.shape
    b = f64(bf(Y)).reshape(n // 32, 32, m)
    amax = np.abs(b).max(1)
    byte = np.clip(np.where(amax > 0, np.frexp(amax)[1] - 1 + 127 - 7, 1), 1, 254)
    codes = (b * np.exp2(127.0 - byte)[:, None, :]).reshape(n, m).astype(np.float32).astype(ml_dtypes.float8_e4m3fn).view(np.uint8)
    words = codes.reshape(n // 512, 128, 4, m).transpose(0, 1, 3, 2)
    return np.ascontiguousarray(words), np.ascontiguousarray(byte.astype(np.uint8).reshape(n // 512, 16, m))


R, L, N, D = 1024, 1024, 512, 1024


def sigmoid(v):
    return 1.0 / (1.0 + np.exp(-v))


def modal_basis(t, om, b):
    a = t[:, None] * om[None, :]
    return b[None, :] * np.exp(-0.1 * a) * np.cos(a)


def setup_inputs():
    s = mx_kscale(L)
    r = mx_kscale(N)
    return {
        "x": bf(np.random.standard_normal((R, L)) * s),
        "t": bf(np.random.uniform(0.0, 1.0, L)),
        "om": bf(np.random.uniform(0.3, 4.5, N)),
        "b": bf(np.random.standard_normal(N) * r),
        "c": bf(np.random.standard_normal((N, D)) / np.sqrt(N) / r[:, None]),
        "win": bf((1.0 + 0.1 * np.random.standard_normal(L)) / s),
        "wg": bf(np.random.standard_normal((L, D)) / np.sqrt(L) / s[:, None]),
    }


def core(x, t, om, b, c, win, wg):
    e = modal_basis(f64(t), f64(om), f64(b))
    ker = mxq(e, 1, "e4m3") @ mxq(f64(c), 0, "e4m3")
    kw = f64(win)[:, None] * ker
    xq = mxq(f64(x), 1, "e4m3")
    u = (xq @ mxq(kw, 0, "e4m3")) / 16.0
    gt = sigmoid(xq @ mxq(f64(wg), 0, "e4m3"))
    return u * gt


def reference(x, t, om, b, c, win, wg):
    R_out = core(x, t, om, b, c, win, wg)
    words, scales = planes(R_out.T)
    return R_out, words, scales

@@ -1,0 +1,433 @@
+import math
+from contextlib import ExitStack
+
+import concourse.mybir as mybir
+from concourse.masks import make_identity
+
+R, L, N, D = 1024, 1024, 512, 1024
+FLOPS = 2 * L * N * D + 2 * 2 * R * L * D
+
+F32 = mybir.dt.float32
+BF16 = mybir.dt.bfloat16
+U32 = mybir.dt.uint32
+I32 = mybir.dt.int32
+U8 = mybir.dt.uint8
+FP8X4 = mybir.dt.float8_e4m3fn_x4
+ALU = mybir.AluOpType
+ACT = mybir.ActivationFunctionType
+
+P = 128
+W = 512
+
+
+def tile_constantqmodalstatespacegatedreadout_x1_kernel(tc, x, t, om, b, c, win, wg, out_0, out_1, out_2):
+    nc = tc.nc
+    with ExitStack() as ctx:
+        keep = ctx.enter_context(tc.tile_pool(name="keep", bufs=1))
+        psum = ctx.enter_context(tc.psum_pool(name="psum", bufs=1))
+        ctx.enter_context(tc.manual_schedule())
+
+        def sb(shape, dtype, name, tag=None, bufs=1):
+            return keep.tile(shape, dtype, name=name, tag=tag or name, bufs=bufs, align_bytes=64)
+
+        def bank(k, shape, dtype, name):
+            return psum.tile(shape, dtype, name=name, tag="bank%d" % k)
+
+        def quantize(codes, scales, grouped):
+            nc.vector.quantize_mx(out=codes.bitcast(FP8X4), scales=scales, in_=grouped)
+
+        def mm(out, lhs, rhs, start, stop):
+            nc.tensor.matmul_mx(out=out, lhsT=lhs[0].bitcast(FP8X4), lhsT_scale=lhs[1],
+                                rhs=rhs[0].bitcast(FP8X4), rhs_scale=rhs[1], start=start, stop=stop)
+
+        def copy(engine, out, in_):
+            if engine == "v":
+                nc.vector.tensor_copy(out=out, in_=in_)
+            elif engine == "s":
+                nc.scalar.copy(out=out, in_=in_)
+            else:
+                nc.gpsimd.tensor_scalar(out=out, in0=in_, scalar1=1.0, scalar2=0.0, op0=ALU.mult, op1=ALU.add)
+
+        def operand(name, width):
+            return (sb([P, width], U32, name + "_codes"), sb([P, width], U8, name + "_scales"))
+
+        def cols(op, start, width):
+            return (op[0][:, start:start + width], op[1][:, start:start + width])
+
+        t_sb = sb([P, 2, 4], BF16, "t_sb")
+        om_sb = sb([P, 4], BF16, "om_sb")
+        b_sb = sb([P, 4], BF16, "b_sb")
+        win_sb = sb([P, 2, 4], BF16, "win_sb")
+        nc.scalar.dma_start(out=t_sb[:], in_=t.rearrange("(g p j) -> p g j", g=2, j=4))
+        nc.scalar.dma_start(out=om_sb[:], in_=om.rearrange("(p j) -> p j", j=4))
+        nc.scalar.dma_start(out=b_sb[:], in_=b.rearrange("(p j) -> p j", j=4))
+        nc.scalar.dma_start(out=win_sb[:], in_=win.rearrange("(g p j) -> p g j", g=2, j=4))
+
+        raw = {}
+        x_raw = {}
+
+        def load_rows(key, rows):
+            raw[key] = sb([P, 4, W], BF16, "raw_%s%d%d" % key)
+            nc.sync.dma_start(out=raw[key][:], in_=rows.rearrange("(p j) d -> p j d", j=4))
+
+        def load_c(h):
+            load_rows(("c", 0, h), c[:, h * W:(h + 1) * W])
+
+        def load_wg(g, h):
+            load_rows(("w", g, h), wg[g * W:(g + 1) * W, h * W:(h + 1) * W])
+
+        def load_x(pair):
+            x_raw[pair] = sb([P, 2 * L], BF16, "x_raw%d" % pair)
+            nc.sync.dma_start(out=x_raw[pair][:].rearrange("p (a l) -> p a l", a=2),
+                              in_=x[pair * 256:(pair + 1) * 256, :].rearrange("(a p) l -> p a l", a=2))
+
+        load_wg(0, 1)
+        load_c(0)
+        load_x(3)
+        load_wg(1, 1)
+        load_x(2)
+        load_wg(1, 0)
+        load_x(1)
+        load_x(0)
+        load_wg(0, 0)
+        load_c(1)
+
+        ident_bf = sb([P, P], BF16, "ident_bf")
+        ident_f = sb([P, P], F32, "ident_f")
+        make_identity(nc, ident_bf[:])
+        make_identity(nc, ident_f[:])
+
+        warm = sb([P, 1], F32, "warm")
+        nc.vector.memset(warm[:], 0.0)
+        nc.scalar.activation(out=warm[:], in_=warm[:], func=ACT.Exp)
+
+        om_decay = sb([P, 4], F32, "om_decay")
+        om_neg = sb([P, 4], F32, "om_neg")
+        nc.vector.tensor_scalar(out=om_decay[:], in0=om_sb[:], scalar1=-0.1, scalar2=None, op0=ALU.mult)
+        nc.vector.tensor_scalar(out=om_neg[:], in0=om_sb[:], scalar1=-1.0, scalar2=None, op0=ALU.mult)
+
+        t_all = bank(0, [P, L], BF16, "t_all")
+        for q in range(8):
+            nc.tensor.transpose(t_all[:, q * P:(q + 1) * P],
+                                t_sb[:, q // 4, q % 4:q % 4 + 1].to_broadcast([P, P]), ident_bf[:])
+
+        decay = sb([P, 4, L], F32, "decay")
+        wave = sb([P, 4, L], F32, "wave")
+
+        grouped = {}
+        q_ops = {}
+        e_op = operand("e", L)
+        x_op = operand("x", 8 * 256)
+        o_scales = sb([P, 2, R], U8, "o_scales")
+        gate = {}
+        res = {}
+        banks = {}
+        rounded = {}
+
+        def exp_step(j):
+            nc.scalar.activation(out=decay[:, j, :], in_=t_all[:], func=ACT.Exp, scale=om_decay[:, j:j + 1])
+
+        def amp_step(j):
+            nc.vector.tensor_scalar(out=decay[:, j, :], in0=decay[:, j, :], scalar1=b_sb[:, j:j + 1], scalar2=None,
+                                    op0=ALU.mult)
+
+        def cos_step(g, j):
+            nc.scalar.activation(out=wave[:, j, g * W:(g + 1) * W], in_=t_all[:, g * W:(g + 1) * W], func=ACT.Sin,
+                                 scale=om_neg[:, j:j + 1], bias=math.pi / 2)
+
+        def e_mult(g):
+            grouped["e", g] = sb([P, W, 4], BF16, "e_grouped%d" % g, tag="grouped", bufs=7)
+            src = "p j (c i) -> p c j i"
+            nc.vector.tensor_tensor(out=grouped["e", g][:].rearrange("p (c i) j -> p c j i", i=4),
+                                    in0=decay[:, :, g * W:(g + 1) * W].rearrange(src, i=4),
+                                    in1=wave[:, :, g * W:(g + 1) * W].rearrange(src, i=4), op=ALU.mult)
+
+        def e_quant(g):
+            quantize(*cols(e_op, g * W, W), grouped["e", g][:].rearrange("p c j -> p (c j)"))
+
+        def interleave(key, a, engine):
+            if key not in grouped:
+                grouped[key] = sb([P, W, 4], BF16, "grouped_%s%d%d" % key, tag="grouped", bufs=7)
+            copy(engine, grouped[key][:, a * 256:(a + 1) * 256, :].rearrange("p (c i) j -> p c j i", i=4),
+                 raw[key][:, :, a * 256:(a + 1) * 256].rearrange("p j (c i) -> p c j i", i=4))
+
+        def quant(key):
+            q_ops[key] = operand("%s%d%d" % key, W)
+            quantize(q_ops[key][0][:], q_ops[key][1][:], grouped[key][:].rearrange("p c j -> p (c j)"))
+
+        def x_turn(i, k):
+            banks["x", i] = bank(k, [P, 2, 2, P], F32, "x_turned%d" % i)
+            words = x_raw[i // 2][:].bitcast(F32)
+            for g in range(2):
+                for u in range(2):
+                    w0 = (i % 2) * W + g * 256
+                    nc.tensor.transpose(banks["x", i][:, g, u, :], words[:, w0 + u:w0 + 256:2], ident_f[:])
+
+        def x_copy(i, engine):
+            grouped["x", i] = sb([P, L], BF16, "x_grouped%d" % i, tag="x_grouped", bufs=8)
+            copy(engine, grouped["x", i][:].bitcast(F32).rearrange("p (g r u) -> p g r u", g=2, u=2),
+                 banks["x", i][:].rearrange("p g u r -> p g r u"))
+
+        def x_quant(i):
+            quantize(*cols(x_op, i * 256, 256), grouped["x", i][:])
+
+        def ker_mm(g, h, s, k):
+            banks["k", g, h, s] = bank(k, [P, 4, P], F32, "ker%d%d%d" % (g, h, s))
+            for j in range(4):
+                mm(banks["k", g, h, s][:, j, :], cols(e_op, g * W + j * P, P), cols(q_ops["c", 0, h], s * P, P), True, True)
+
+        def kw_mult(g, h, s):
+            if ("k", g, h) not in grouped:
+                grouped["k", g, h] = sb([P, W, 4], BF16, "grouped_k%d%d" % (g, h), tag="grouped", bufs=7)
+            nc.vector.tensor_tensor(out=grouped["k", g, h][:, s * P:(s + 1) * P, :],
+                                    in0=banks["k", g, h, s][:].rearrange("p j d -> p d j"),
+                                    in1=win_sb[:, g, :].unsqueeze(1).to_broadcast([P, P, 4]), op=ALU.mult)
+
+        def x_product(kind, i, h, k):
+            banks[kind, i, h] = bank(k, [P, W], F32, "acc_%s%d%d" % (kind, i, h))
+            for g in range(2):
+                mm(banks[kind, i, h][:], cols(x_op, i * 256 + g * P, P), cols(q_ops[kind, g, h], 0, W), g == 0, g == 1)
+
+        def gate_step(i, h):
+            gate[i, h] = sb([P, W], F32, "gate%d%d" % (i, h))
+            nc.scalar.activation(out=gate[i, h][:], in_=banks["w", i, h][:], func=ACT.Sigmoid)
+
+        def result(i, h):
+            res[i, h] = gate[i, h]
+            nc.vector.scalar_tensor_tensor(out=res[i, h][:], in0=banks["k", i, h][:], scalar=1.0 / 16.0,
+                                           in1=gate[i, h][:], op0=ALU.mult, op1=ALU.mult)
+            nc.sync.dma_start(out=out_0[i * P:(i + 1) * P, h * W:(h + 1) * W], in_=res[i, h][:])
+
+        def round_step(i, h, engine):
+            rounded[i, h] = sb([P, W], BF16, "rounded%d%d" % (i, h), tag="rounded", bufs=16)
+            copy(engine, rounded[i, h][:].rearrange("r (u p e) -> r u p e", u=2, e=2),
+                 res[i, h][:].rearrange("r (p u e) -> r u p e", u=2, e=2))
+
+        def o_turn(pair, h, k):
+            banks["o", pair, h] = bank(k, [P, 2, 2, P], F32, "o_turned%d%d" % (pair, h))
+            for a in range(2):
+                words = rounded[2 * pair + a, h][:].bitcast(F32)
+                for u in range(2):
+                    nc.tensor.transpose(banks["o", pair, h][:, a, u, :], words[:, u * P:(u + 1) * P], ident_f[:])
+
+        def o_copy(pair, h, engine):
+            grouped["o", pair, h] = sb([P, L], BF16, "o_grouped%d%d" % (pair, h), tag="x_grouped", bufs=8)
+            copy(engine, grouped["o", pair, h][:].bitcast(F32).rearrange("p (a r u) -> p a r u", a=2, u=2),
+                 banks["o", pair, h][:].rearrange("p a u r -> p a r u"))
+
+        def o_quant(pair, h):
+            codes = sb([P, 256], U32, "o_codes%d%d" % (pair, h))
+            quantize(codes[:], o_scales[:, h, pair * 256:(pair + 1) * 256], grouped["o", pair, h][:])
+            words_out = out_1[h].rearrange("p m t -> p (m t)").bitcast(I32)
+            nc.sync.dma_start(out=words_out[:, pair * 256:(pair + 1) * 256], in_=codes[:].bitcast(I32))
+
+        def store_scales():
+            for q in range(4):
+                engine = nc.sync if q % 2 == 0 else nc.scalar
+                engine.dma_start(out=out_2[:, 4 * q:4 * q + 4, :].rearrange("h q m -> q h m").bitcast(I32),
+                                 in_=o_scales[32 * q:32 * q + 4, :, :].bitcast(I32))
+
+
+        interleave(("w", 0, 1), 0, "v")
+        exp_step(0)
+        interleave(("w", 0, 1), 1, "v")
+        interleave(("c", 0, 0), 0, "v")
+        exp_step(1)
+        quant(("w", 0, 1))
+        x_turn(7, 1)
+        exp_step(3)
+        amp_step(0)
+        interleave(("c", 0, 0), 1, "v")
+        x_turn(6, 2)
+        exp_step(2)
+        amp_step(3)
+        interleave(("w", 1, 1), 0, "v")
+        x_turn(5, 3)
+        interleave(("w", 1, 1), 1, "v")
+        amp_step(2)
+        quant(("w", 1, 1))
+        cos_step(1, 1)
+        x_copy(6, "v")
+        cos_step(1, 2)
+        x_turn(2, 4)
+        amp_step(1)
+        cos_step(1, 3)
+        interleave(("w", 1, 0), 1, "v")
+        cos_step(1, 0)
+        x_turn(1, 5)
+        quant(("c", 0, 0))
+        x_copy(5, "s")
+        x_quant(6)
+        e_mult(1)
+        cos_step(0, 1)
+        x_turn(0, 6)
+        x_copy(1, "s")
+        x_turn(3, 7)
+        cos_step(0, 0)
+        cos_step(0, 3)
+        x_copy(0, "s")
+        x_quant(5)
+        e_quant(1)
+        cos_step(0, 2)
+        interleave(("w", 0, 0), 1, "v")
+        ker_mm(1, 0, 3, 2)
+        interleave(("w", 1, 0), 0, "s")
+        e_mult(0)
+        ker_mm(1, 0, 2, 3)
+        x_copy(2, "s")
+        x_product("w", 6, 1, 5)
+        x_copy(3, "s")
+        x_copy(7, "s")
+        ker_mm(1, 0, 0, 6)
+        x_quant(3)
+        x_turn(4, 0)
+        interleave(("c", 0, 1), 1, "s")
+        e_quant(0)
+        x_quant(2)
+        ker_mm(0, 0, 0, 4)
+        kw_mult(1, 0, 2)
+        interleave(("c", 0, 1), 0, "s")
+        x_product("w", 2, 1, 7)
+        kw_mult(1, 0, 0)
+        x_quant(7)
+        x_copy(4, "s")
+        ker_mm(1, 0, 1, 1)
+        quant(("w", 1, 0))
+        x_product("w", 3, 1, 3)
+        interleave(("w", 0, 0), 0, "s")
+        kw_mult(0, 0, 0)
+        ker_mm(0, 0, 3, 6)
+        ker_mm(0, 0, 1, 0)
+        quant(("c", 0, 1))
+        ker_mm(0, 0, 2, 4)
+        kw_mult(1, 0, 1)
+        kw_mult(1, 0, 3)
+        ker_mm(1, 1, 3, 1)
+        kw_mult(0, 0, 2)
+        x_product("w", 5, 1, 2)
+        gate_step(6, 1)
+        quant(("w", 0, 0))
+        x_product("w", 7, 1, 4)
+        gate_step(2, 1)
+        x_quant(4)
+        x_product("w", 5, 0, 5)
+        kw_mult(0, 0, 3)
+        gate_step(7, 1)
+        x_product("w", 2, 0, 7)
+        kw_mult(0, 0, 1)
+        gate_step(5, 0)
+        ker_mm(0, 1, 2, 6)
+        quant(("k", 1, 0))
+        ker_mm(1, 1, 2, 4)
+        gate_step(2, 0)
+        x_product("w", 4, 0, 0)
+        x_quant(1)
+        gate_step(5, 1)
+        x_quant(0)
+        x_product("w", 7, 0, 5)
+        kw_mult(1, 1, 3)
+        gate_step(4, 0)
+        ker_mm(1, 1, 0, 7)
+        quant(("k", 0, 0))
+        x_product("w", 3, 0, 2)
+        kw_mult(0, 1, 2)
+        ker_mm(0, 1, 0, 1)
+        gate_step(3, 0)
+        x_product("k", 2, 0, 0)
+        kw_mult(1, 1, 2)
+        gate_step(3, 1)
+        x_product("k", 5, 0, 6)
+        result(2, 0)
+        ker_mm(0, 1, 1, 2)
+        result(5, 0)
+        ker_mm(1, 1, 1, 4)
+        round_step(2, 0, "s")
+        x_product("w", 1, 1, 3)
+        kw_mult(1, 1, 0)
+        round_step(5, 0, "s")
+        x_product("w", 1, 0, 0)
+        kw_mult(0, 1, 0)
+        gate_step(7, 0)
+        ker_mm(0, 1, 3, 6)
+        kw_mult(1, 1, 1)
+        x_product("w", 0, 0, 7)
+        gate_step(1, 1)
+        kw_mult(0, 1, 1)
+        x_product("k", 4, 0, 1)
+        gate_step(0, 0)
+        kw_mult(0, 1, 3)
+        x_product("w", 0, 1, 5)
+        gate_step(1, 0)
+        quant(("k", 1, 1))
+        x_product("k", 1, 0, 4)
+        gate_step(0, 1)
+        x_product("w", 6, 0, 3)
+        quant(("k", 0, 1))
+        x_product("k", 6, 0, 2)
+        result(1, 0)
+        gate_step(6, 0)
+        x_product("k", 2, 1, 7)
+        result(4, 0)
+        round_step(1, 0, "s")
+        x_product("k", 7, 1, 6)
+        result(2, 1)
+        x_product("k", 3, 1, 0)
+        result(7, 1)
+        round_step(2, 1, "s")
+        x_product("k", 7, 0, 5)
+        result(3, 1)
+        round_step(4, 0, "s")
+        x_product("k", 0, 0, 4)
+        result(6, 0)
+        round_step(7, 1, "s")
+        x_product("k", 3, 0, 3)
+        result(7, 0)
+        round_step(3, 1, "s")
+        x_product("k", 6, 1, 1)
+        result(0, 0)
+        round_step(7, 0, "s")
+        x_product("k", 0, 1, 7)
+        result(6, 1)
+        round_step(6, 0, "s")
+        o_turn(1, 1, 6)
+        round_step(0, 0, "v")
+        o_turn(2, 0, 0)
+        round_step(6, 1, "s")
+        result(3, 0)
+        o_turn(3, 0, 2)
+        x_product("w", 4, 1, 5)
+        o_copy(2, 0, "s")
+        o_copy(1, 1, "v")
+        round_step(3, 0, "s")
+        x_product("k", 5, 1, 4)
+        o_quant(2, 0)
+        result(0, 1)
+        gate_step(4, 1)
+        x_product("k", 1, 1, 1)
+        result(5, 1)
+        round_step(0, 1, "s")
+        x_product("k", 4, 1, 3)
+        result(1, 1)
+        o_copy(3, 0, "s")
+        o_turn(0, 0, 0)
+        result(4, 1)
+        o_turn(3, 1, 6)
+        o_copy(0, 0, "s")
+        o_turn(1, 0, 7)
+        round_step(1, 1, "v")
+        round_step(4, 1, "v")
+        o_copy(3, 1, "s")
+        o_turn(0, 1, 5)
+        round_step(5, 1, "v")
+        o_quant(3, 0)
+        o_copy(1, 0, "s")
+        o_turn(2, 1, 4)
+        o_quant(0, 0)
+        o_copy(0, 1, "s")
+        o_quant(3, 1)
+        o_quant(1, 0)
+        o_copy(2, 1, "s")
+        o_quant(1, 1)
+        o_quant(0, 1)
+        o_quant(2, 1)
+        store_scales()

@@ -58,7 +58,7 @@ def tile_constantqmodalstatespacegatedreadout_x1_kernel(tc, x, t, om, b, c, win,
         om_sb = sb([P, 4], BF16, "om_sb")
         b_sb = sb([P, 4], BF16, "b_sb")
         win_sb = sb([P, 2, 4], BF16, "win_sb")
-        nc.scalar.dma_start(out=t_sb[:], in_=t.rearrange("(g p j) -> p g j", g=2, j=4))
+        nc.sync.dma_start(out=t_sb[:], in_=t.rearrange("(g p j) -> p g j", g=2, j=4))
         nc.scalar.dma_start(out=om_sb[:], in_=om.rearrange("(p j) -> p j", j=4))
         nc.scalar.dma_start(out=b_sb[:], in_=b.rearrange("(p j) -> p j", j=4))
         nc.scalar.dma_start(out=win_sb[:], in_=win.rearrange("(g p j) -> p g j", g=2, j=4))
@@ -69,6 +69,13 @@ def tile_constantqmodalstatespacegatedreadout_x1_kernel(tc, x, t, om, b, c, win,
         def load_rows(key, rows):
             raw[key] = sb([P, 4, W], BF16, "raw_%s%d%d" % key)
             nc.sync.dma_start(out=raw[key][:], in_=rows.rearrange("(p j) d -> p j d", j=4))
+
+        def load_c_half(a):
+            if ("c", 0, 0) not in raw:
+                raw["c", 0, 0] = [None, None]
+            raw["c", 0, 0][a] = sb([P, 4, 256], BF16, "raw_c_first%d" % a)
+            nc.sync.dma_start(out=raw["c", 0, 0][a][:],
+                              in_=c[:, a * 256:(a + 1) * 256].rearrange("(p j) d -> p j d", j=4))
 
         def load_c(h):
             load_rows(("c", 0, h), c[:, h * W:(h + 1) * W])
@@ -81,16 +88,17 @@ def tile_constantqmodalstatespacegatedreadout_x1_kernel(tc, x, t, om, b, c, win,
             nc.sync.dma_start(out=x_raw[pair][:].rearrange("p (a l) -> p a l", a=2),
                               in_=x[pair * 256:(pair + 1) * 256, :].rearrange("(a p) l -> p a l", a=2))
 
-        load_wg(0, 1)
-        load_c(0)
-        load_x(3)
-        load_wg(1, 1)
-        load_x(2)
         load_wg(1, 0)
-        load_x(1)
-        load_x(0)
-        load_wg(0, 0)
         load_c(1)
+        load_x(0)
+        load_c_half(0)
+        load_x(3)
+        load_c_half(1)
+        load_wg(0, 1)
+        load_x(2)
+        load_x(1)
+        load_wg(0, 0)
+        load_wg(1, 1)
 
         ident_bf = sb([P, P], BF16, "ident_bf")
         ident_f = sb([P, P], F32, "ident_f")
@@ -99,48 +107,55 @@ def tile_constantqmodalstatespacegatedreadout_x1_kernel(tc, x, t, om, b, c, win,
 
         warm = sb([P, 1], F32, "warm")
         nc.vector.memset(warm[:], 0.0)
-        nc.scalar.activation(out=warm[:], in_=warm[:], func=ACT.Exp)
+        nc.scalar.activation(out=warm[:], in_=warm[:], func=ACT.Sin)
 
         om_decay = sb([P, 4], F32, "om_decay")
         om_neg = sb([P, 4], F32, "om_neg")
-        nc.vector.tensor_scalar(out=om_decay[:], in0=om_sb[:], scalar1=-0.1, scalar2=None, op0=ALU.mult)
-        nc.vector.tensor_scalar(out=om_neg[:], in0=om_sb[:], scalar1=-1.0, scalar2=None, op0=ALU.mult)
+        win_scaled = sb([P, 2, 4], F32, "win_scaled")
+        nc.gpsimd.tensor_scalar(out=om_neg[:], in0=om_sb[:], scalar1=-1.0, scalar2=0.0, op0=ALU.mult, op1=ALU.add)
+        nc.gpsimd.tensor_scalar(out=om_decay[:], in0=om_sb[:], scalar1=-0.1, scalar2=0.0, op0=ALU.mult, op1=ALU.add)
+        nc.gpsimd.tensor_scalar(out=win_scaled[:], in0=win_sb[:], scalar1=1.0 / 32.0, scalar2=0.0, op0=ALU.mult,
+                                op1=ALU.add)
 
-        t_all = bank(0, [P, L], BF16, "t_all")
-        for q in range(8):
-            nc.tensor.transpose(t_all[:, q * P:(q + 1) * P],
-                                t_sb[:, q // 4, q % 4:q % 4 + 1].to_broadcast([P, P]), ident_bf[:])
+        t_all = [bank(g, [P, W], BF16, "t_all%d" % g) for g in range(2)]
+        for g in range(2):
+            for j in range(4):
+                nc.tensor.transpose(t_all[g][:, j * P:(j + 1) * P],
+                                    t_sb[:, g, j:j + 1].to_broadcast([P, P]), ident_bf[:])
 
-        decay = sb([P, 4, L], F32, "decay")
         wave = sb([P, 4, L], F32, "wave")
+        decay = [sb([P, 4, W], F32, "decay%d" % g) for g in range(2)]
 
         grouped = {}
         q_ops = {}
         e_op = operand("e", L)
         x_op = operand("x", 8 * 256)
-        o_scales = sb([P, 2, R], U8, "o_scales")
+        o_scales = [sb([P, R], U8, "o_scales%d" % h) for h in range(2)]
+        o_codes = {}
         gate = {}
         res = {}
         banks = {}
         rounded = {}
 
-        def exp_step(j):
-            nc.scalar.activation(out=decay[:, j, :], in_=t_all[:], func=ACT.Exp, scale=om_decay[:, j:j + 1])
-
-        def amp_step(j):
-            nc.vector.tensor_scalar(out=decay[:, j, :], in0=decay[:, j, :], scalar1=b_sb[:, j:j + 1], scalar2=None,
-                                    op0=ALU.mult)
-
         def cos_step(g, j):
-            nc.scalar.activation(out=wave[:, j, g * W:(g + 1) * W], in_=t_all[:, g * W:(g + 1) * W], func=ACT.Sin,
+            nc.scalar.activation(out=wave[:, j, g * W:(g + 1) * W], in_=t_all[g][:], func=ACT.Sin,
                                  scale=om_neg[:, j:j + 1], bias=math.pi / 2)
 
-        def e_mult(g):
-            grouped["e", g] = sb([P, W, 4], BF16, "e_grouped%d" % g, tag="grouped", bufs=7)
+        def amp_step(j):
+            nc.vector.tensor_scalar(out=wave[:, j, :], in0=wave[:, j, :], scalar1=b_sb[:, j:j + 1], scalar2=None,
+                                    op0=ALU.mult)
+
+        def exp_step(g, j):
+            nc.scalar.activation(out=decay[g][:, j, :], in_=t_all[g][:], func=ACT.Exp, scale=om_decay[:, j:j + 1])
+
+        def e_mult(g, a):
+            if ("e", g) not in grouped:
+                grouped["e", g] = sb([P, W, 4], BF16, "e_grouped%d" % g, tag="grouped", bufs=7)
             src = "p j (c i) -> p c j i"
-            nc.vector.tensor_tensor(out=grouped["e", g][:].rearrange("p (c i) j -> p c j i", i=4),
-                                    in0=decay[:, :, g * W:(g + 1) * W].rearrange(src, i=4),
-                                    in1=wave[:, :, g * W:(g + 1) * W].rearrange(src, i=4), op=ALU.mult)
+            c0 = a * 256
+            nc.vector.tensor_tensor(out=grouped["e", g][:, c0:c0 + 256, :].rearrange("p (c i) j -> p c j i", i=4),
+                                    in0=decay[g][:, :, c0:c0 + 256].rearrange(src, i=4),
+                                    in1=wave[:, :, g * W + c0:g * W + c0 + 256].rearrange(src, i=4), op=ALU.mult)
 
         def e_quant(g):
             quantize(*cols(e_op, g * W, W), grouped["e", g][:].rearrange("p c j -> p (c j)"))
@@ -148,8 +163,9 @@ def tile_constantqmodalstatespacegatedreadout_x1_kernel(tc, x, t, om, b, c, win,
         def interleave(key, a, engine):
             if key not in grouped:
                 grouped[key] = sb([P, W, 4], BF16, "grouped_%s%d%d" % key, tag="grouped", bufs=7)
+            src = raw[key][a][:] if key == ("c", 0, 0) else raw[key][:, :, a * 256:(a + 1) * 256]
             copy(engine, grouped[key][:, a * 256:(a + 1) * 256, :].rearrange("p (c i) j -> p c j i", i=4),
-                 raw[key][:, :, a * 256:(a + 1) * 256].rearrange("p j (c i) -> p c j i", i=4))
+                 src.rearrange("p j (c i) -> p c j i", i=4))
 
         def quant(key):
             q_ops[key] = operand("%s%d%d" % key, W)
@@ -164,7 +180,7 @@ def tile_constantqmodalstatespacegatedreadout_x1_kernel(tc, x, t, om, b, c, win,
                     nc.tensor.transpose(banks["x", i][:, g, u, :], words[:, w0 + u:w0 + 256:2], ident_f[:])
 
         def x_copy(i, engine):
-            grouped["x", i] = sb([P, L], BF16, "x_grouped%d" % i, tag="x_grouped", bufs=8)
+            grouped["x", i] = sb([P, L], BF16, "x_grouped%d" % i, tag="x_grouped", bufs=9)
             copy(engine, grouped["x", i][:].bitcast(F32).rearrange("p (g r u) -> p g r u", g=2, u=2),
                  banks["x", i][:].rearrange("p g u r -> p g r u"))
 
@@ -181,7 +197,7 @@ def tile_constantqmodalstatespacegatedreadout_x1_kernel(tc, x, t, om, b, c, win,
                 grouped["k", g, h] = sb([P, W, 4], BF16, "grouped_k%d%d" % (g, h), tag="grouped", bufs=7)
             nc.vector.tensor_tensor(out=grouped["k", g, h][:, s * P:(s + 1) * P, :],
                                     in0=banks["k", g, h, s][:].rearrange("p j d -> p d j"),
-                                    in1=win_sb[:, g, :].unsqueeze(1).to_broadcast([P, P, 4]), op=ALU.mult)
+                                    in1=win_scaled[:, g, :].unsqueeze(1).to_broadcast([P, P, 4]), op=ALU.mult)
 
         def x_product(kind, i, h, k):
             banks[kind, i, h] = bank(k, [P, W], F32, "acc_%s%d%d" % (kind, i, h))
@@ -190,12 +206,14 @@ def tile_constantqmodalstatespacegatedreadout_x1_kernel(tc, x, t, om, b, c, win,
 
         def gate_step(i, h):
             gate[i, h] = sb([P, W], F32, "gate%d%d" % (i, h))
-            nc.scalar.activation(out=gate[i, h][:], in_=banks["w", i, h][:], func=ACT.Sigmoid)
+            nc.scalar.activation(out=gate[i, h][:], in_=banks["w", i, h][:], func=ACT.Tanh, scale=0.5)
 
         def result(i, h):
             res[i, h] = gate[i, h]
-            nc.vector.scalar_tensor_tensor(out=res[i, h][:], in0=banks["k", i, h][:], scalar=1.0 / 16.0,
-                                           in1=gate[i, h][:], op0=ALU.mult, op1=ALU.mult)
+            nc.vector.scalar_tensor_tensor(out=res[i, h][:], in0=gate[i, h][:], scalar=1.0,
+                                           in1=banks["k", i, h][:], op0=ALU.add, op1=ALU.mult)
+
+        def store_result(i, h):
             nc.sync.dma_start(out=out_0[i * P:(i + 1) * P, h * W:(h + 1) * W], in_=res[i, h][:])
 
         def round_step(i, h, engine):
@@ -203,231 +221,272 @@ def tile_constantqmodalstatespacegatedreadout_x1_kernel(tc, x, t, om, b, c, win,
             copy(engine, rounded[i, h][:].rearrange("r (u p e) -> r u p e", u=2, e=2),
                  res[i, h][:].rearrange("r (p u e) -> r u p e", u=2, e=2))
 
-        def o_turn(pair, h, k):
-            banks["o", pair, h] = bank(k, [P, 2, 2, P], F32, "o_turned%d%d" % (pair, h))
-            for a in range(2):
-                words = rounded[2 * pair + a, h][:].bitcast(F32)
+        def o_turn(i, n, h, k):
+            banks["o", i, h] = bank(k, [P, n, 2, P], F32, "o_turned%d%d" % (i, h))
+            for a in range(n):
+                words = rounded[i + a, h][:].bitcast(F32)
                 for u in range(2):
-                    nc.tensor.transpose(banks["o", pair, h][:, a, u, :], words[:, u * P:(u + 1) * P], ident_f[:])
+                    nc.tensor.transpose(banks["o", i, h][:, a, u, :], words[:, u * P:(u + 1) * P], ident_f[:])
 
-        def o_copy(pair, h, engine):
-            grouped["o", pair, h] = sb([P, L], BF16, "o_grouped%d%d" % (pair, h), tag="x_grouped", bufs=8)
-            copy(engine, grouped["o", pair, h][:].bitcast(F32).rearrange("p (a r u) -> p a r u", a=2, u=2),
-                 banks["o", pair, h][:].rearrange("p a u r -> p a r u"))
+        def o_copy(i, n, h, engine):
+            grouped["o", i, h] = sb([P, n * W], BF16, "o_grouped%d%d" % (i, h), tag="x_grouped", bufs=9)
+            copy(engine, grouped["o", i, h][:].bitcast(F32).rearrange("p (a r u) -> p a r u", a=n, u=2),
+                 banks["o", i, h][:].rearrange("p a u r -> p a r u"))
 
-        def o_quant(pair, h):
-            codes = sb([P, 256], U32, "o_codes%d%d" % (pair, h))
-            quantize(codes[:], o_scales[:, h, pair * 256:(pair + 1) * 256], grouped["o", pair, h][:])
+        def o_quant(i, n, h):
+            o_codes[i, h] = sb([P, n * P], U32, "o_codes%d%d" % (i, h))
+            quantize(o_codes[i, h][:], o_scales[h][:, i * P:(i + n) * P], grouped["o", i, h][:])
+
+        def store_codes(i, n, h):
             words_out = out_1[h].rearrange("p m t -> p (m t)").bitcast(I32)
-            nc.sync.dma_start(out=words_out[:, pair * 256:(pair + 1) * 256], in_=codes[:].bitcast(I32))
+            nc.sync.dma_start(out=words_out[:, i * P:(i + n) * P], in_=o_codes[i, h][:].bitcast(I32))
 
-        def store_scales():
-            for q in range(4):
-                engine = nc.sync if q % 2 == 0 else nc.scalar
-                engine.dma_start(out=out_2[:, 4 * q:4 * q + 4, :].rearrange("h q m -> q h m").bitcast(I32),
-                                 in_=o_scales[32 * q:32 * q + 4, :, :].bitcast(I32))
+        def store_scales(h, q, engine):
+            queue = nc.sync if engine == "sp" else nc.scalar
+            queue.dma_start(out=out_2[h, 4 * q:4 * q + 4, :].bitcast(I32),
+                            in_=o_scales[h][32 * q:32 * q + 4, :].bitcast(I32))
 
-
-        interleave(("w", 0, 1), 0, "v")
-        exp_step(0)
-        interleave(("w", 0, 1), 1, "v")
-        interleave(("c", 0, 0), 0, "v")
-        exp_step(1)
-        quant(("w", 0, 1))
-        x_turn(7, 1)
-        exp_step(3)
-        amp_step(0)
-        interleave(("c", 0, 0), 1, "v")
-        x_turn(6, 2)
-        exp_step(2)
-        amp_step(3)
-        interleave(("w", 1, 1), 0, "v")
-        x_turn(5, 3)
-        interleave(("w", 1, 1), 1, "v")
-        amp_step(2)
-        quant(("w", 1, 1))
-        cos_step(1, 1)
-        x_copy(6, "v")
-        cos_step(1, 2)
-        x_turn(2, 4)
-        amp_step(1)
-        cos_step(1, 3)
-        interleave(("w", 1, 0), 1, "v")
-        cos_step(1, 0)
-        x_turn(1, 5)
-        quant(("c", 0, 0))
-        x_copy(5, "s")
-        x_quant(6)
-        e_mult(1)
-        cos_step(0, 1)
-        x_turn(0, 6)
-        x_copy(1, "s")
-        x_turn(3, 7)
-        cos_step(0, 0)
         cos_step(0, 3)
-        x_copy(0, "s")
-        x_quant(5)
-        e_quant(1)
-        cos_step(0, 2)
-        interleave(("w", 0, 0), 1, "v")
-        ker_mm(1, 0, 3, 2)
-        interleave(("w", 1, 0), 0, "s")
-        e_mult(0)
-        ker_mm(1, 0, 2, 3)
-        x_copy(2, "s")
-        x_product("w", 6, 1, 5)
-        x_copy(3, "s")
-        x_copy(7, "s")
-        ker_mm(1, 0, 0, 6)
-        x_quant(3)
-        x_turn(4, 0)
-        interleave(("c", 0, 1), 1, "s")
-        e_quant(0)
-        x_quant(2)
-        ker_mm(0, 0, 0, 4)
-        kw_mult(1, 0, 2)
-        interleave(("c", 0, 1), 0, "s")
-        x_product("w", 2, 1, 7)
-        kw_mult(1, 0, 0)
-        x_quant(7)
-        x_copy(4, "s")
-        ker_mm(1, 0, 1, 1)
+        cos_step(0, 1)
+        cos_step(1, 3)
+        cos_step(1, 0)
+        x_turn(1, 2)
+        interleave(("w", 1, 0), 1, "v")
+        interleave(("w", 1, 0), 0, "v")
+        interleave(("c", 0, 1), 1, "v")
+        cos_step(1, 2)
         quant(("w", 1, 0))
-        x_product("w", 3, 1, 3)
-        interleave(("w", 0, 0), 0, "s")
-        kw_mult(0, 0, 0)
-        ker_mm(0, 0, 3, 6)
-        ker_mm(0, 0, 1, 0)
+        amp_step(3)
+        cos_step(1, 1)
+        cos_step(0, 2)
+        cos_step(0, 0)
+        x_turn(0, 3)
+        exp_step(0, 2)
+        x_turn(7, 4)
+        interleave(("c", 0, 1), 0, "v")
+        amp_step(1)
+        exp_step(0, 0)
         quant(("c", 0, 1))
-        ker_mm(0, 0, 2, 4)
-        kw_mult(1, 0, 1)
-        kw_mult(1, 0, 3)
-        ker_mm(1, 1, 3, 1)
-        kw_mult(0, 0, 2)
-        x_product("w", 5, 1, 2)
-        gate_step(6, 1)
-        quant(("w", 0, 0))
-        x_product("w", 7, 1, 4)
-        gate_step(2, 1)
-        x_quant(4)
-        x_product("w", 5, 0, 5)
-        kw_mult(0, 0, 3)
-        gate_step(7, 1)
-        x_product("w", 2, 0, 7)
-        kw_mult(0, 0, 1)
-        gate_step(5, 0)
-        ker_mm(0, 1, 2, 6)
-        quant(("k", 1, 0))
-        ker_mm(1, 1, 2, 4)
-        gate_step(2, 0)
-        x_product("w", 4, 0, 0)
-        x_quant(1)
-        gate_step(5, 1)
+        interleave(("c", 0, 0), 0, "v")
+        x_turn(6, 5)
+        amp_step(2)
+        exp_step(0, 1)
+        exp_step(0, 3)
+        interleave(("c", 0, 0), 1, "v")
+        exp_step(1, 3)
+        interleave(("w", 0, 1), 0, "v")
+        amp_step(0)
+        quant(("c", 0, 0))
+        x_turn(5, 6)
+        exp_step(1, 2)
+        x_copy(5, "s")
+        e_mult(0, 1)
+        exp_step(1, 0)
+        x_turn(2, 7)
+        e_mult(0, 0)
+        x_quant(5)
+        x_copy(0, "s")
+        e_quant(0)
+        exp_step(1, 1)
+        x_copy(1, "s")
+        x_turn(4, 0)
+        x_turn(3, 6)
+        ker_mm(0, 0, 1, 3)
         x_quant(0)
-        x_product("w", 7, 0, 5)
-        kw_mult(1, 1, 3)
-        gate_step(4, 0)
-        ker_mm(1, 1, 0, 7)
-        quant(("k", 0, 0))
-        x_product("w", 3, 0, 2)
-        kw_mult(0, 1, 2)
+        e_mult(1, 0)
+        interleave(("w", 0, 0), 0, "s")
+        e_mult(1, 1)
+        ker_mm(0, 0, 0, 1)
+        kw_mult(0, 0, 0)
+        x_copy(3, "s")
+        ker_mm(0, 0, 3, 2)
+        ker_mm(0, 1, 2, 6)
         ker_mm(0, 1, 0, 1)
-        gate_step(3, 0)
-        x_product("k", 2, 0, 0)
-        kw_mult(1, 1, 2)
-        gate_step(3, 1)
-        x_product("k", 5, 0, 6)
-        result(2, 0)
-        ker_mm(0, 1, 1, 2)
-        result(5, 0)
-        ker_mm(1, 1, 1, 4)
-        round_step(2, 0, "s")
-        x_product("w", 1, 1, 3)
-        kw_mult(1, 1, 0)
-        round_step(5, 0, "s")
-        x_product("w", 1, 0, 0)
+        x_copy(7, "s")
+        x_quant(7)
+        x_copy(2, "s")
+        e_quant(1)
+        x_copy(6, "s")
+        kw_mult(0, 0, 1)
+        ker_mm(0, 1, 1, 4)
+        x_copy(4, "s")
+        ker_mm(1, 0, 3, 7)
         kw_mult(0, 1, 0)
-        gate_step(7, 0)
-        ker_mm(0, 1, 3, 6)
-        kw_mult(1, 1, 1)
-        x_product("w", 0, 0, 7)
-        gate_step(1, 1)
-        kw_mult(0, 1, 1)
-        x_product("k", 4, 0, 1)
-        gate_step(0, 0)
+        kw_mult(1, 0, 3)
+        ker_mm(1, 1, 0, 5)
+        interleave(("w", 0, 0), 1, "s")
+        kw_mult(1, 1, 0)
+        quant(("w", 0, 0))
+        kw_mult(0, 1, 2)
+        ker_mm(1, 1, 3, 3)
+        ker_mm(0, 0, 2, 0)
+        kw_mult(0, 0, 2)
+        ker_mm(1, 0, 2, 1)
+        interleave(("w", 1, 1), 0, "s")
+        x_quant(4)
+        ker_mm(0, 1, 3, 7)
+        x_product("w", 0, 0, 5)
         kw_mult(0, 1, 3)
-        x_product("w", 0, 1, 5)
+        x_product("w", 7, 0, 6)
+        interleave(("w", 0, 1), 1, "s")
+        x_product("w", 5, 0, 0)
+        gate_step(0, 0)
+        kw_mult(1, 1, 3)
+        interleave(("w", 1, 1), 1, "s")
+        x_product("w", 4, 0, 5)
+        gate_step(5, 0)
+        gate_step(4, 0)
+        kw_mult(0, 1, 1)
+        quant(("w", 0, 1))
+        x_quant(1)
+        ker_mm(1, 0, 1, 7)
+        ker_mm(1, 0, 0, 3)
+        ker_mm(1, 1, 2, 4)
+        quant(("w", 1, 1))
+        gate_step(7, 0)
+        kw_mult(1, 1, 2)
+        ker_mm(1, 1, 1, 0)
+        x_product("w", 1, 0, 5)
+        x_product("w", 4, 1, 6)
+        x_product("w", 1, 1, 4)
         gate_step(1, 0)
-        quant(("k", 1, 1))
-        x_product("k", 1, 0, 4)
-        gate_step(0, 1)
-        x_product("w", 6, 0, 3)
-        quant(("k", 0, 1))
-        x_product("k", 6, 0, 2)
-        result(1, 0)
-        gate_step(6, 0)
-        x_product("k", 2, 1, 7)
-        result(4, 0)
-        round_step(1, 0, "s")
-        x_product("k", 7, 1, 6)
-        result(2, 1)
-        x_product("k", 3, 1, 0)
-        result(7, 1)
-        round_step(2, 1, "s")
-        x_product("k", 7, 0, 5)
-        result(3, 1)
-        round_step(4, 0, "s")
-        x_product("k", 0, 0, 4)
-        result(6, 0)
-        round_step(7, 1, "s")
-        x_product("k", 3, 0, 3)
-        result(7, 0)
-        round_step(3, 1, "s")
-        x_product("k", 6, 1, 1)
-        result(0, 0)
-        round_step(7, 0, "s")
-        x_product("k", 0, 1, 7)
-        result(6, 1)
-        round_step(6, 0, "s")
-        o_turn(1, 1, 6)
-        round_step(0, 0, "v")
-        o_turn(2, 0, 0)
-        round_step(6, 1, "s")
-        result(3, 0)
-        o_turn(3, 0, 2)
-        x_product("w", 4, 1, 5)
-        o_copy(2, 0, "s")
-        o_copy(1, 1, "v")
-        round_step(3, 0, "s")
-        x_product("k", 5, 1, 4)
-        o_quant(2, 0)
-        result(0, 1)
+        x_product("w", 5, 1, 5)
+        x_quant(6)
         gate_step(4, 1)
-        x_product("k", 1, 1, 1)
-        result(5, 1)
-        round_step(0, 1, "s")
-        x_product("k", 4, 1, 3)
-        result(1, 1)
-        o_copy(3, 0, "s")
-        o_turn(0, 0, 0)
+        x_product("w", 6, 1, 6)
+        kw_mult(0, 0, 3)
+        kw_mult(1, 1, 1)
+        quant(("k", 0, 1))
+        gate_step(5, 1)
+        x_quant(3)
+        x_product("w", 7, 1, 2)
+        gate_step(6, 1)
+        quant(("k", 1, 1))
+        kw_mult(1, 0, 0)
+        x_product("w", 3, 1, 0)
+        x_product("k", 4, 1, 5)
+        gate_step(7, 1)
+        x_product("k", 6, 1, 6)
+        x_product("k", 7, 1, 3)
+        kw_mult(1, 0, 1)
+        x_product("k", 5, 1, 2)
         result(4, 1)
-        o_turn(3, 1, 6)
-        o_copy(0, 0, "s")
-        o_turn(1, 0, 7)
-        round_step(1, 1, "v")
-        round_step(4, 1, "v")
-        o_copy(3, 1, "s")
-        o_turn(0, 1, 5)
-        round_step(5, 1, "v")
-        o_quant(3, 0)
-        o_copy(1, 0, "s")
-        o_turn(2, 1, 4)
-        o_quant(0, 0)
-        o_copy(0, 1, "s")
-        o_quant(3, 1)
-        o_quant(1, 0)
-        o_copy(2, 1, "s")
-        o_quant(1, 1)
-        o_quant(0, 1)
-        o_quant(2, 1)
-        store_scales()
+        x_product("k", 1, 1, 7)
+        x_quant(2)
+        gate_step(3, 1)
+        result(6, 1)
+        store_result(6, 1)
+        result(7, 1)
+        gate_step(1, 1)
+        x_product("w", 0, 1, 0)
+        result(5, 1)
+        store_result(5, 1)
+        store_result(7, 1)
+        round_step(4, 1, "s")
+        store_result(4, 1)
+        round_step(6, 1, "s")
+        kw_mult(1, 0, 2)
+        round_step(7, 1, "s")
+        result(1, 1)
+        quant(("k", 1, 0))
+        quant(("k", 0, 0))
+        x_product("k", 2, 1, 5)
+        store_result(1, 1)
+        x_product("w", 2, 1, 4)
+        o_turn(7, 1, 1, 6)
+        round_step(5, 1, "s")
+        gate_step(0, 1)
+        gate_step(2, 1)
+        o_turn(4, 2, 1, 3)
+        result(2, 1)
+        o_turn(6, 1, 1, 2)
+        store_result(2, 1)
+        x_product("k", 0, 1, 1)
+        result(0, 1)
+        store_result(0, 1)
+        o_copy(7, 1, 1, "s")
+        x_product("k", 3, 1, 7)
+        result(3, 1)
+        x_product("k", 4, 0, 0)
+        o_quant(7, 1, 1)
+        x_product("k", 7, 0, 4)
+        result(4, 0)
+        store_result(3, 1)
+        store_codes(7, 1, 1)
+        x_product("k", 5, 0, 6)
+        o_copy(4, 2, 1, "s")
+        o_quant(4, 2, 1)
+        o_copy(6, 1, 1, "s")
+        store_result(4, 0)
+        store_codes(4, 2, 1)
+        result(5, 0)
+        round_step(2, 1, "s")
+        round_step(3, 1, "s")
+        x_product("k", 1, 0, 3)
+        result(7, 0)
+        store_result(5, 0)
+        round_step(0, 1, "s")
+        o_quant(6, 1, 1)
+        store_result(7, 0)
+        x_product("k", 0, 0, 5)
+        result(0, 0)
+        o_turn(2, 2, 1, 2)
+        round_step(1, 1, "s")
+        o_turn(0, 2, 1, 1)
+        round_step(4, 0, "s")
+        store_codes(6, 1, 1)
+        result(1, 0)
+        round_step(7, 0, "v")
+        store_result(1, 0)
+        x_product("w", 6, 0, 7)
+        o_copy(2, 2, 1, "s")
+        o_copy(0, 2, 1, "s")
+        o_quant(2, 2, 1)
+        store_codes(2, 2, 1)
+        o_quant(0, 2, 1)
+        store_scales(1, 1, "sp")
+        round_step(0, 0, "v")
+        round_step(5, 0, "s")
+        x_product("w", 2, 0, 0)
+        store_result(0, 0)
+        store_codes(0, 2, 1)
+        gate_step(6, 0)
+        x_product("k", 6, 0, 6)
+        store_scales(1, 0, "sp")
+        round_step(1, 0, "v")
+        x_product("w", 3, 0, 4)
+        result(6, 0)
+        store_result(6, 0)
+        gate_step(2, 0)
+        x_product("k", 2, 0, 5)
+        result(2, 0)
+        x_product("k", 3, 0, 2)
+        gate_step(3, 0)
+        result(3, 0)
+        o_turn(4, 2, 0, 3)
+        round_step(3, 0, "v")
+        round_step(6, 0, "s")
+        round_step(2, 0, "s")
+        store_result(2, 0)
+        store_result(3, 0)
+        o_turn(6, 2, 0, 1)
+        store_scales(1, 3, "s")
+        store_scales(1, 2, "s")
+        o_copy(6, 2, 0, "v")
+        o_quant(6, 2, 0)
+        store_codes(6, 2, 0)
+        o_copy(4, 2, 0, "s")
+        o_quant(4, 2, 0)
+        store_codes(4, 2, 0)
+        o_turn(0, 2, 0, 7)
+        o_copy(0, 2, 0, "s")
+        o_quant(0, 2, 0)
+        o_turn(2, 2, 0, 0)
+        store_codes(0, 2, 0)
+        o_copy(2, 2, 0, "s")
+        o_quant(2, 2, 0)
+        store_codes(2, 2, 0)
+        store_scales(0, 2, "s")
+        store_scales(0, 3, "sp")
+        store_scales(0, 0, "s")
+        store_scales(0, 1, "s")

@@ -70,12 +70,12 @@ def tile_constantqmodalstatespacegatedreadout_x1_kernel(tc, x, t, om, b, c, win,
             raw[key] = sb([P, 4, W], BF16, "raw_%s%d%d" % key)
             nc.sync.dma_start(out=raw[key][:], in_=rows.rearrange("(p j) d -> p j d", j=4))
 
-        def load_c_half(a):
-            if ("c", 0, 0) not in raw:
-                raw["c", 0, 0] = [None, None]
-            raw["c", 0, 0][a] = sb([P, 4, 256], BF16, "raw_c_first%d" % a)
-            nc.sync.dma_start(out=raw["c", 0, 0][a][:],
-                              in_=c[:, a * 256:(a + 1) * 256].rearrange("(p j) d -> p j d", j=4))
+        def load_wg_half(a):
+            if ("w", 1, 1) not in raw:
+                raw["w", 1, 1] = [None, None]
+            raw["w", 1, 1][a] = sb([P, 4, 256], BF16, "raw_w_first%d" % a)
+            nc.sync.dma_start(out=raw["w", 1, 1][a][:],
+                              in_=wg[W:, W + a * 256:W + (a + 1) * 256].rearrange("(p j) d -> p j d", j=4))
 
         def load_c(h):
             load_rows(("c", 0, h), c[:, h * W:(h + 1) * W])
@@ -88,17 +88,17 @@ def tile_constantqmodalstatespacegatedreadout_x1_kernel(tc, x, t, om, b, c, win,
             nc.sync.dma_start(out=x_raw[pair][:].rearrange("p (a l) -> p a l", a=2),
                               in_=x[pair * 256:(pair + 1) * 256, :].rearrange("(a p) l -> p a l", a=2))
 
-        load_wg(1, 0)
-        load_c(1)
-        load_x(0)
-        load_c_half(0)
-        load_x(3)
-        load_c_half(1)
         load_wg(0, 1)
-        load_x(2)
+        load_x(0)
         load_x(1)
+        load_c(1)
+        load_x(2)
+        load_wg_half(1)
+        load_wg_half(0)
         load_wg(0, 0)
-        load_wg(1, 1)
+        load_x(3)
+        load_c(0)
+        load_wg(1, 0)
 
         ident_bf = sb([P, P], BF16, "ident_bf")
         ident_f = sb([P, P], F32, "ident_f")
@@ -124,7 +124,7 @@ def tile_constantqmodalstatespacegatedreadout_x1_kernel(tc, x, t, om, b, c, win,
                                     t_sb[:, g, j:j + 1].to_broadcast([P, P]), ident_bf[:])
 
         wave = sb([P, 4, L], F32, "wave")
-        decay = [sb([P, 4, W], F32, "decay%d" % g) for g in range(2)]
+        decay = {}
 
         grouped = {}
         q_ops = {}
@@ -133,6 +133,7 @@ def tile_constantqmodalstatespacegatedreadout_x1_kernel(tc, x, t, om, b, c, win,
         o_scales = [sb([P, R], U8, "o_scales%d" % h) for h in range(2)]
         o_codes = {}
         gate = {}
+        pair_tile = {}
         res = {}
         banks = {}
         rounded = {}
@@ -145,16 +146,20 @@ def tile_constantqmodalstatespacegatedreadout_x1_kernel(tc, x, t, om, b, c, win,
             nc.vector.tensor_scalar(out=wave[:, j, :], in0=wave[:, j, :], scalar1=b_sb[:, j:j + 1], scalar2=None,
                                     op0=ALU.mult)
 
-        def exp_step(g, j):
-            nc.scalar.activation(out=decay[g][:, j, :], in_=t_all[g][:], func=ACT.Exp, scale=om_decay[:, j:j + 1])
+        def exp_step(g, a, n, j):
+            if (g, a) not in decay:
+                decay[g, a] = sb([P, 4, n * 256], F32, "decay%d%d" % (g, a))
+            nc.scalar.activation(out=decay[g, a][:, j, :], in_=t_all[g][:, a * 256:(a + n) * 256], func=ACT.Exp,
+                                 scale=om_decay[:, j:j + 1])
 
         def e_mult(g, a):
             if ("e", g) not in grouped:
                 grouped["e", g] = sb([P, W, 4], BF16, "e_grouped%d" % g, tag="grouped", bufs=7)
             src = "p j (c i) -> p c j i"
             c0 = a * 256
+            part = decay[g, a][:] if (g, a) in decay and g == 1 else decay[g, 0][:, :, c0:c0 + 256]
             nc.vector.tensor_tensor(out=grouped["e", g][:, c0:c0 + 256, :].rearrange("p (c i) j -> p c j i", i=4),
-                                    in0=decay[g][:, :, c0:c0 + 256].rearrange(src, i=4),
+                                    in0=part.rearrange(src, i=4),
                                     in1=wave[:, :, g * W + c0:g * W + c0 + 256].rearrange(src, i=4), op=ALU.mult)
 
         def e_quant(g):
@@ -163,7 +168,7 @@ def tile_constantqmodalstatespacegatedreadout_x1_kernel(tc, x, t, om, b, c, win,
         def interleave(key, a, engine):
             if key not in grouped:
                 grouped[key] = sb([P, W, 4], BF16, "grouped_%s%d%d" % key, tag="grouped", bufs=7)
-            src = raw[key][a][:] if key == ("c", 0, 0) else raw[key][:, :, a * 256:(a + 1) * 256]
+            src = raw[key][a][:] if key == ("w", 1, 1) else raw[key][:, :, a * 256:(a + 1) * 256]
             copy(engine, grouped[key][:, a * 256:(a + 1) * 256, :].rearrange("p (c i) j -> p c j i", i=4),
                  src.rearrange("p j (c i) -> p c j i", i=4))
 
@@ -205,21 +210,24 @@ def tile_constantqmodalstatespacegatedreadout_x1_kernel(tc, x, t, om, b, c, win,
                 mm(banks[kind, i, h][:], cols(x_op, i * 256 + g * P, P), cols(q_ops[kind, g, h], 0, W), g == 0, g == 1)
 
         def gate_step(i, h):
-            gate[i, h] = sb([P, W], F32, "gate%d%d" % (i, h))
-            nc.scalar.activation(out=gate[i, h][:], in_=banks["w", i, h][:], func=ACT.Tanh, scale=0.5)
+            if (i // 2, h) not in pair_tile:
+                pair_tile[i // 2, h] = sb([P, 2, W], F32, "gate%d%d" % (i // 2, h))
+            gate[i, h] = pair_tile[i // 2, h][:, i % 2, :]
+            nc.scalar.activation(out=gate[i, h], in_=banks["w", i, h][:], func=ACT.Tanh, scale=0.5)
 
         def result(i, h):
             res[i, h] = gate[i, h]
-            nc.vector.scalar_tensor_tensor(out=res[i, h][:], in0=gate[i, h][:], scalar=1.0,
+            nc.vector.scalar_tensor_tensor(out=res[i, h], in0=gate[i, h], scalar=1.0,
                                            in1=banks["k", i, h][:], op0=ALU.add, op1=ALU.mult)
 
-        def store_result(i, h):
-            nc.sync.dma_start(out=out_0[i * P:(i + 1) * P, h * W:(h + 1) * W], in_=res[i, h][:])
+        def store_result(pair, h):
+            rows = out_0[pair * 256:(pair + 1) * 256, h * W:(h + 1) * W]
+            nc.sync.dma_start(out=rows.rearrange("(a p) d -> p a d", a=2), in_=pair_tile[pair, h][:])
 
         def round_step(i, h, engine):
             rounded[i, h] = sb([P, W], BF16, "rounded%d%d" % (i, h), tag="rounded", bufs=16)
             copy(engine, rounded[i, h][:].rearrange("r (u p e) -> r u p e", u=2, e=2),
-                 res[i, h][:].rearrange("r (p u e) -> r u p e", u=2, e=2))
+                 res[i, h].rearrange("r (p u e) -> r u p e", u=2, e=2))
 
         def o_turn(i, n, h, k):
             banks["o", i, h] = bank(k, [P, n, 2, P], F32, "o_turned%d%d" % (i, h))
@@ -247,246 +255,242 @@ def tile_constantqmodalstatespacegatedreadout_x1_kernel(tc, x, t, om, b, c, win,
                             in_=o_scales[h][32 * q:32 * q + 4, :].bitcast(I32))
 
         cos_step(0, 3)
-        cos_step(0, 1)
-        cos_step(1, 3)
-        cos_step(1, 0)
-        x_turn(1, 2)
-        interleave(("w", 1, 0), 1, "v")
-        interleave(("w", 1, 0), 0, "v")
-        interleave(("c", 0, 1), 1, "v")
-        cos_step(1, 2)
-        quant(("w", 1, 0))
-        amp_step(3)
-        cos_step(1, 1)
-        cos_step(0, 2)
-        cos_step(0, 0)
-        x_turn(0, 3)
-        exp_step(0, 2)
-        x_turn(7, 4)
-        interleave(("c", 0, 1), 0, "v")
-        amp_step(1)
-        exp_step(0, 0)
-        quant(("c", 0, 1))
-        interleave(("c", 0, 0), 0, "v")
-        x_turn(6, 5)
-        amp_step(2)
-        exp_step(0, 1)
-        exp_step(0, 3)
-        interleave(("c", 0, 0), 1, "v")
-        exp_step(1, 3)
         interleave(("w", 0, 1), 0, "v")
-        amp_step(0)
-        quant(("c", 0, 0))
-        x_turn(5, 6)
-        exp_step(1, 2)
-        x_copy(5, "s")
-        e_mult(0, 1)
-        exp_step(1, 0)
-        x_turn(2, 7)
-        e_mult(0, 0)
-        x_quant(5)
-        x_copy(0, "s")
-        e_quant(0)
-        exp_step(1, 1)
-        x_copy(1, "s")
-        x_turn(4, 0)
-        x_turn(3, 6)
-        ker_mm(0, 0, 1, 3)
-        x_quant(0)
-        e_mult(1, 0)
-        interleave(("w", 0, 0), 0, "s")
-        e_mult(1, 1)
-        ker_mm(0, 0, 0, 1)
-        kw_mult(0, 0, 0)
-        x_copy(3, "s")
-        ker_mm(0, 0, 3, 2)
-        ker_mm(0, 1, 2, 6)
-        ker_mm(0, 1, 0, 1)
-        x_copy(7, "s")
-        x_quant(7)
-        x_copy(2, "s")
-        e_quant(1)
-        x_copy(6, "s")
-        kw_mult(0, 0, 1)
-        ker_mm(0, 1, 1, 4)
-        x_copy(4, "s")
-        ker_mm(1, 0, 3, 7)
-        kw_mult(0, 1, 0)
-        kw_mult(1, 0, 3)
-        ker_mm(1, 1, 0, 5)
-        interleave(("w", 0, 0), 1, "s")
-        kw_mult(1, 1, 0)
-        quant(("w", 0, 0))
-        kw_mult(0, 1, 2)
-        ker_mm(1, 1, 3, 3)
-        ker_mm(0, 0, 2, 0)
-        kw_mult(0, 0, 2)
-        ker_mm(1, 0, 2, 1)
-        interleave(("w", 1, 1), 0, "s")
-        x_quant(4)
-        ker_mm(0, 1, 3, 7)
-        x_product("w", 0, 0, 5)
-        kw_mult(0, 1, 3)
-        x_product("w", 7, 0, 6)
-        interleave(("w", 0, 1), 1, "s")
-        x_product("w", 5, 0, 0)
-        gate_step(0, 0)
-        kw_mult(1, 1, 3)
-        interleave(("w", 1, 1), 1, "s")
-        x_product("w", 4, 0, 5)
-        gate_step(5, 0)
-        gate_step(4, 0)
-        kw_mult(0, 1, 1)
+        cos_step(1, 3)
+        interleave(("w", 0, 1), 1, "v")
+        amp_step(3)
+        cos_step(1, 0)
         quant(("w", 0, 1))
+        cos_step(0, 0)
+        amp_step(0)
+        cos_step(1, 1)
+        x_turn(1, 2)
+        x_copy(1, "v")
+        x_turn(0, 3)
+        cos_step(0, 1)
+        amp_step(1)
+        cos_step(0, 2)
+        cos_step(1, 2)
+        exp_step(0, 0, 2, 2)
+        exp_step(0, 0, 2, 3)
+        exp_step(1, 0, 1, 0)
+        x_turn(3, 4)
+        x_turn(5, 5)
+        exp_step(0, 0, 2, 0)
+        x_turn(4, 6)
         x_quant(1)
-        ker_mm(1, 0, 1, 7)
-        ker_mm(1, 0, 0, 3)
-        ker_mm(1, 1, 2, 4)
+        amp_step(2)
+        exp_step(0, 0, 2, 1)
+        interleave(("c", 0, 1), 1, "v")
+        interleave(("w", 1, 1), 1, "v")
+        x_copy(0, "s")
+        x_copy(3, "s")
+        interleave(("c", 0, 1), 0, "v")
+        interleave(("w", 1, 1), 0, "v")
+        quant(("c", 0, 1))
         quant(("w", 1, 1))
-        gate_step(7, 0)
-        kw_mult(1, 1, 2)
-        ker_mm(1, 1, 1, 0)
-        x_product("w", 1, 0, 5)
-        x_product("w", 4, 1, 6)
-        x_product("w", 1, 1, 4)
-        gate_step(1, 0)
-        x_product("w", 5, 1, 5)
+        exp_step(1, 1, 1, 2)
+        x_turn(6, 7)
+        x_copy(6, "s")
+        e_mult(0, 1)
+        exp_step(1, 1, 1, 3)
+        exp_step(1, 1, 1, 0)
+        x_turn(2, 2)
+        exp_step(1, 1, 1, 1)
+        x_quant(0)
+        x_copy(5, "s")
+        exp_step(1, 0, 1, 1)
+        x_turn(7, 0)
+        e_mult(0, 0)
         x_quant(6)
-        gate_step(4, 1)
-        x_product("w", 6, 1, 6)
-        kw_mult(0, 0, 3)
-        kw_mult(1, 1, 1)
-        quant(("k", 0, 1))
-        gate_step(5, 1)
-        x_quant(3)
-        x_product("w", 7, 1, 2)
-        gate_step(6, 1)
-        quant(("k", 1, 1))
-        kw_mult(1, 0, 0)
-        x_product("w", 3, 1, 0)
-        x_product("k", 4, 1, 5)
-        gate_step(7, 1)
-        x_product("k", 6, 1, 6)
-        x_product("k", 7, 1, 3)
-        kw_mult(1, 0, 1)
-        x_product("k", 5, 1, 2)
-        result(4, 1)
-        x_product("k", 1, 1, 7)
-        x_quant(2)
-        gate_step(3, 1)
-        result(6, 1)
-        store_result(6, 1)
-        result(7, 1)
-        gate_step(1, 1)
-        x_product("w", 0, 1, 0)
-        result(5, 1)
-        store_result(5, 1)
-        store_result(7, 1)
-        round_step(4, 1, "s")
-        store_result(4, 1)
-        round_step(6, 1, "s")
-        kw_mult(1, 0, 2)
-        round_step(7, 1, "s")
-        result(1, 1)
-        quant(("k", 1, 0))
-        quant(("k", 0, 0))
-        x_product("k", 2, 1, 5)
-        store_result(1, 1)
-        x_product("w", 2, 1, 4)
-        o_turn(7, 1, 1, 6)
-        round_step(5, 1, "s")
+        e_quant(0)
+        x_product("w", 0, 1, 3)
+        exp_step(1, 0, 1, 3)
+        ker_mm(0, 1, 2, 4)
+        exp_step(1, 0, 1, 2)
+        ker_mm(0, 1, 0, 7)
+        ker_mm(0, 1, 3, 5)
+        e_mult(1, 1)
+        x_copy(2, "s")
+        x_copy(7, "s")
         gate_step(0, 1)
+        e_mult(1, 0)
+        ker_mm(0, 1, 1, 1)
+        x_quant(5)
+        x_quant(2)
+        e_quant(1)
+        x_quant(3)
+        x_product("w", 5, 1, 2)
+        ker_mm(1, 1, 3, 0)
+        kw_mult(0, 1, 0)
+        kw_mult(1, 1, 3)
+        x_product("w", 1, 1, 3)
+        interleave(("c", 0, 0), 1, "s")
+        kw_mult(0, 1, 1)
+        interleave(("c", 0, 0), 0, "s")
+        x_product("w", 6, 1, 7)
+        kw_mult(0, 1, 2)
+        gate_step(5, 1)
+        ker_mm(1, 1, 1, 0)
+        ker_mm(1, 1, 2, 2)
+        gate_step(6, 1)
+        quant(("c", 0, 0))
+        x_product("w", 2, 1, 1)
+        ker_mm(1, 1, 0, 7)
+        ker_mm(1, 0, 2, 4)
+        x_copy(4, "s")
+        x_product("w", 3, 1, 6)
+        kw_mult(0, 1, 3)
+        ker_mm(0, 0, 3, 5)
+        x_quant(4)
+        x_quant(7)
+        interleave(("w", 0, 0), 1, "s")
+        kw_mult(1, 1, 2)
+        x_product("w", 7, 1, 2)
+        gate_step(1, 1)
         gate_step(2, 1)
-        o_turn(4, 2, 1, 3)
-        result(2, 1)
-        o_turn(6, 1, 1, 2)
-        store_result(2, 1)
-        x_product("k", 0, 1, 1)
+        interleave(("w", 1, 0), 0, "s")
+        gate_step(7, 1)
+        ker_mm(0, 0, 1, 3)
+        kw_mult(1, 1, 0)
+        ker_mm(1, 0, 1, 1)
+        kw_mult(1, 1, 1)
+        ker_mm(0, 0, 0, 7)
+        quant(("k", 0, 1))
+        quant(("k", 1, 1))
+        x_product("w", 4, 1, 0)
+        kw_mult(0, 0, 0)
+        kw_mult(0, 0, 3)
+        x_product("k", 7, 1, 2)
+        result(7, 1)
+        interleave(("w", 1, 0), 1, "s")
+        quant(("w", 1, 0))
+        gate_step(4, 1)
+        x_product("k", 1, 1, 7)
+        x_product("k", 0, 1, 5)
         result(0, 1)
-        store_result(0, 1)
-        o_copy(7, 1, 1, "s")
-        x_product("k", 3, 1, 7)
-        result(3, 1)
-        x_product("k", 4, 0, 0)
-        o_quant(7, 1, 1)
-        x_product("k", 7, 0, 4)
-        result(4, 0)
+        x_product("k", 4, 1, 2)
+        result(1, 1)
+        round_step(7, 1, "g")
+        interleave(("w", 0, 0), 0, "s")
+        quant(("w", 0, 0))
+        gate_step(3, 1)
+        x_product("k", 2, 1, 0)
+        x_product("k", 6, 1, 5)
+        x_product("k", 5, 1, 7)
+        result(6, 1)
+        round_step(6, 1, "s")
+        result(5, 1)
         store_result(3, 1)
-        store_codes(7, 1, 1)
-        x_product("k", 5, 0, 6)
-        o_copy(4, 2, 1, "s")
-        o_quant(4, 2, 1)
-        o_copy(6, 1, 1, "s")
-        store_result(4, 0)
-        store_codes(4, 2, 1)
-        result(5, 0)
-        round_step(2, 1, "s")
-        round_step(3, 1, "s")
-        x_product("k", 1, 0, 3)
-        result(7, 0)
-        store_result(5, 0)
-        round_step(0, 1, "s")
-        o_quant(6, 1, 1)
-        store_result(7, 0)
-        x_product("k", 0, 0, 5)
-        result(0, 0)
-        o_turn(2, 2, 1, 2)
-        round_step(1, 1, "s")
-        o_turn(0, 2, 1, 1)
-        round_step(4, 0, "s")
-        store_codes(6, 1, 1)
-        result(1, 0)
-        round_step(7, 0, "v")
-        store_result(1, 0)
-        x_product("w", 6, 0, 7)
-        o_copy(2, 2, 1, "s")
+        x_product("w", 3, 0, 6)
+        x_product("w", 4, 0, 5)
+        x_product("k", 3, 1, 7)
+        result(4, 1)
+        round_step(1, 1, "g")
+        ker_mm(1, 0, 3, 2)
+        gate_step(3, 0)
+        round_step(0, 1, "g")
+        round_step(4, 1, "g")
+        gate_step(4, 0)
+        round_step(5, 1, "s")
+        result(2, 1)
+        result(3, 1)
+        x_product("w", 1, 0, 6)
+        store_result(0, 1)
+        o_turn(0, 2, 1, 0)
+        gate_step(1, 0)
+        kw_mult(1, 0, 3)
         o_copy(0, 2, 1, "s")
+        o_turn(6, 2, 1, 5)
+        kw_mult(1, 0, 2)
+        round_step(2, 1, "g")
+        ker_mm(0, 0, 2, 7)
+        x_product("w", 0, 0, 2)
+        o_copy(6, 2, 1, "s")
+        gate_step(0, 0)
+        store_result(2, 1)
+        kw_mult(0, 0, 1)
+        kw_mult(0, 0, 2)
+        kw_mult(1, 0, 1)
+        ker_mm(1, 0, 0, 6)
+        round_step(3, 1, "g")
+        kw_mult(1, 0, 0)
+        quant(("k", 0, 0))
+        o_turn(2, 2, 1, 4)
+        o_turn(4, 2, 1, 0)
+        o_copy(2, 2, 1, "s")
+        store_result(1, 1)
+        o_copy(4, 2, 1, "s")
+        quant(("k", 1, 0))
         o_quant(2, 2, 1)
-        store_codes(2, 2, 1)
+        o_quant(6, 2, 1)
+        x_product("w", 2, 0, 3)
+        x_product("w", 6, 0, 5)
         o_quant(0, 2, 1)
-        store_scales(1, 1, "sp")
-        round_step(0, 0, "v")
-        round_step(5, 0, "s")
-        x_product("w", 2, 0, 0)
-        store_result(0, 0)
-        store_codes(0, 2, 1)
+        x_product("w", 5, 0, 7)
+        gate_step(2, 0)
         gate_step(6, 0)
+        gate_step(5, 0)
+        x_product("k", 2, 0, 2)
+        x_product("k", 3, 0, 1)
+        o_quant(4, 2, 1)
+        store_scales(1, 2, "s")
+        result(2, 0)
         x_product("k", 6, 0, 6)
+        store_codes(2, 2, 1)
+        store_scales(1, 3, "s")
+        result(3, 0)
+        round_step(3, 0, "s")
+        x_product("k", 5, 0, 4)
+        store_codes(6, 2, 1)
+        result(6, 0)
+        result(5, 0)
+        store_codes(0, 2, 1)
+        x_product("k", 4, 0, 0)
+        x_product("k", 1, 0, 3)
+        store_codes(4, 2, 1)
+        round_step(2, 0, "g")
+        store_result(1, 0)
+        store_scales(1, 1, "sp")
+        result(4, 0)
+        round_step(5, 0, "s")
+        result(1, 0)
+        x_product("k", 0, 0, 5)
+        round_step(6, 0, "g")
+        o_turn(6, 1, 0, 7)
+        o_turn(2, 2, 0, 2)
+        o_copy(6, 1, 0, "s")
+        result(0, 0)
         store_scales(1, 0, "sp")
         round_step(1, 0, "v")
-        x_product("w", 3, 0, 4)
-        result(6, 0)
-        store_result(6, 0)
-        gate_step(2, 0)
-        x_product("k", 2, 0, 5)
-        result(2, 0)
-        x_product("k", 3, 0, 2)
-        gate_step(3, 0)
-        result(3, 0)
-        o_turn(4, 2, 0, 3)
-        round_step(3, 0, "v")
-        round_step(6, 0, "s")
-        round_step(2, 0, "s")
+        o_quant(6, 1, 0)
+        o_copy(2, 2, 0, "s")
+        round_step(4, 0, "v")
+        x_product("w", 7, 0, 1)
+        gate_step(7, 0)
+        o_quant(2, 2, 0)
+        round_step(0, 0, "s")
         store_result(2, 0)
-        store_result(3, 0)
-        o_turn(6, 2, 0, 1)
-        store_scales(1, 3, "s")
-        store_scales(1, 2, "s")
-        o_copy(6, 2, 0, "v")
-        o_quant(6, 2, 0)
-        store_codes(6, 2, 0)
+        store_result(0, 0)
+        x_product("k", 7, 0, 6)
+        result(7, 0)
+        round_step(7, 0, "v")
+        o_turn(4, 2, 0, 4)
+        o_turn(0, 2, 0, 0)
+        o_turn(7, 1, 0, 3)
         o_copy(4, 2, 0, "s")
+        store_codes(6, 1, 0)
         o_quant(4, 2, 0)
-        store_codes(4, 2, 0)
-        o_turn(0, 2, 0, 7)
+        store_codes(2, 2, 0)
+        store_result(3, 0)
         o_copy(0, 2, 0, "s")
         o_quant(0, 2, 0)
-        o_turn(2, 2, 0, 0)
-        store_codes(0, 2, 0)
-        o_copy(2, 2, 0, "s")
-        o_quant(2, 2, 0)
-        store_codes(2, 2, 0)
-        store_scales(0, 2, "s")
-        store_scales(0, 3, "sp")
-        store_scales(0, 0, "s")
+        o_copy(7, 1, 0, "s")
+        o_quant(7, 1, 0)
         store_scales(0, 1, "s")
+        store_codes(4, 2, 0)
+        store_codes(0, 2, 0)
+        store_codes(7, 1, 0)
+        store_scales(0, 2, "s")
+        store_scales(0, 3, "s")
+        store_scales(0, 0, "sp")

@@ -17,28 +17,78 @@ ALU = mybir.AluOpType
 ACT = mybir.ActivationFunctionType
 
 P = 128
-W = 512
+PACK = 4
+K_PASS = P * PACK
+GROUPS = L // K_PASS
+HALF = 512
+PART = 256
+ROW_TILES = R // P
+BANKS = 8
+
+PAIRS = [(i, 2) for i in range(0, ROW_TILES, 2)]
+PLANE_UNITS = [PAIRS, PAIRS[:-1] + [(ROW_TILES - 2, 1), (ROW_TILES - 1, 1)]]
+
+ORDER = """
+cos cos cos cos cos cos w_group.0:v w_group.0:v amplitude cos cos exp exp w_group.0:v exp exp exp
+w_group.0:v exp x_turn x_turn amplitude x_turn amplitude x_turn exp w_quant.0 c_group.0:v x_turn x_turn exp
+x_copy:s x_copy:s exp c_group.0:v exp exp exp amplitude exp c_quant.0 x_turn e_product exp exp exp x_copy:s
+x_copy:s e_product x_quant e_quant e_product ker.0 x_wg.0 ker.0 ker.0 x_wg.0 x_copy:s x_turn kw_product.0
+e_product kw_product.0 x_copy:s ker.0 e_quant kw_product.0 c_group.1:s ker.0 x_quant ker.0 x_wg.0
+kw_product.0 kw_product.0 c_group.1:s x_copy:s x_wg.0 c_quant.1 ker.0 x_quant ker.0 tanh.0 tanh.0 ker.1
+x_wg.0 kw_product.0 tanh.0 kw_product.0 x_copy:s kw_product.0 tanh.0 x_quant x_wg.0 tanh.0 kw_quant.0 ker.1
+ker.1 ker.1 kw_product.1 kw_product.1 x_wg.0 tanh.0 x_wg.0 x_kw.0 result.0 w_group.1:s x_kw.0 x_kw.0
+round_result.0:g x_kw.0 result.0 x_kw.0 x_kw.0 round_result.0:g kw_product.1 result.0 result.0 w_group.1:s
+w_group.1:s x_kw.0 w_group.1:s round_result.0:g result.0 w_quant.1 tanh.0 ker.1 ker.1 ker.1 tanh.0 result.0
+round_result.0:s round_result.0:s result.0 x_kw.0 x_wg.1 round_result.0:g result.0 round_result.0:g x_wg.1
+tanh.1 store_result.0 x_wg.1 tanh.1 kw_product.1 kw_product.1 round_result.0:g tanh.1 ker.1 out_turn.0
+store_result.0 store_result.0 store_result.0 out_copy.0:s out_turn.0 out_turn.0 out_turn.0 out_copy.0:s
+out_copy.0:s x_wg.1 out_copy.0:s x_wg.1 tanh.1 kw_product.1 kw_product.1 x_wg.1 kw_product.1 kw_quant.1
+x_wg.1 out_quant.0 x_kw.1 store_scales.0:y x_kw.1 x_kw.1 result.1 result.1 tanh.1 x_kw.1 tanh.1 tanh.1
+store_scales.0:s store_scales.0:y round_result.1:g store_scales.0:s result.1 result.1 x_kw.1 x_kw.1
+store_codes.0 round_result.1:g result.1 store_result.1 round_result.1:s result.1 out_turn.1 round_result.1:s
+out_turn.1 out_copy.1:v store_result.1 out_quant.1 out_copy.1:s store_result.1 x_wg.1 out_quant.1
+round_result.1:g x_kw.1 x_kw.1 store_codes.1 round_result.1:s store_codes.1 result.1 tanh.1 result.1
+out_turn.1 round_result.1:v out_turn.1 store_result.1 round_result.1:v out_copy.1:s out_quant.1 out_turn.1
+out_copy.1:v out_quant.1 out_copy.1:s out_quant.1 store_codes.1 store_codes.1 store_scales.1:s store_codes.1
+store_scales.1:s store_scales.1:y store_scales.1:s
+"""
 
 
 def tile_constantqmodalstatespacegatedreadout_x1_kernel(tc, x, t, om, b, c, win, wg, out_0, out_1, out_2):
     nc = tc.nc
     with ExitStack() as ctx:
-        keep = ctx.enter_context(tc.tile_pool(name="keep", bufs=1))
+        sbuf = ctx.enter_context(tc.tile_pool(name="sbuf", bufs=1))
         psum = ctx.enter_context(tc.psum_pool(name="psum", bufs=1))
         ctx.enter_context(tc.manual_schedule())
 
         def sb(shape, dtype, name, tag=None, bufs=1):
-            return keep.tile(shape, dtype, name=name, tag=tag or name, bufs=bufs, align_bytes=64)
+            return sbuf.tile(shape, dtype, name=name, tag=tag or name, bufs=bufs, align_bytes=64)
 
-        def bank(k, shape, dtype, name):
-            return psum.tile(shape, dtype, name=name, tag="bank%d" % k)
+        free_banks = list(range(BANKS))
+        held = {}
 
-        def quantize(codes, scales, grouped):
-            nc.vector.quantize_mx(out=codes.bitcast(FP8X4), scales=scales, in_=grouped)
+        def take_bank(key, shape, dtype):
+            number = free_banks[0]
+            free_banks.remove(number)
+            held[key] = (number, psum.tile(shape, dtype, name="psum_%s_%d_%d" % key, tag="bank%d" % number))
+            return held[key][1]
 
-        def mm(out, lhs, rhs, start, stop):
-            nc.tensor.matmul_mx(out=out, lhsT=lhs[0].bitcast(FP8X4), lhsT_scale=lhs[1],
-                                rhs=rhs[0].bitcast(FP8X4), rhs_scale=rhs[1], start=start, stop=stop)
+        def last_read(key):
+            free_banks.append(held[key][0])
+            return held[key][1]
+
+        def operand(name, columns):
+            return (sb([P, columns], U32, name + "_codes"), sb([P, columns], U8, name + "_scales"))
+
+        def columns_of(op, start, count):
+            return (op[0][:, start:start + count], op[1][:, start:start + count])
+
+        def quantize(op, grouped):
+            nc.vector.quantize_mx(out=op[0].bitcast(FP8X4), scales=op[1], in_=grouped)
+
+        def matmul(out, stationary, moving, start, stop):
+            nc.tensor.matmul_mx(out=out, lhsT=stationary[0].bitcast(FP8X4), lhsT_scale=stationary[1],
+                                rhs=moving[0].bitcast(FP8X4), rhs_scale=moving[1], start=start, stop=stop)
 
         def copy(engine, out, in_):
             if engine == "v":
@@ -46,451 +96,259 @@ def tile_constantqmodalstatespacegatedreadout_x1_kernel(tc, x, t, om, b, c, win,
             elif engine == "s":
                 nc.scalar.copy(out=out, in_=in_)
             else:
-                nc.gpsimd.tensor_scalar(out=out, in0=in_, scalar1=1.0, scalar2=0.0, op0=ALU.mult, op1=ALU.add)
+                times(out, in_, 1.0)
 
-        def operand(name, width):
-            return (sb([P, width], U32, name + "_codes"), sb([P, width], U8, name + "_scales"))
+        def times(out, in_, factor):
+            nc.gpsimd.tensor_scalar(out=out, in0=in_, scalar1=factor, scalar2=0.0, op0=ALU.mult, op1=ALU.add)
 
-        def cols(op, start, width):
-            return (op[0][:, start:start + width], op[1][:, start:start + width])
-
-        t_sb = sb([P, 2, 4], BF16, "t_sb")
-        om_sb = sb([P, 4], BF16, "om_sb")
-        b_sb = sb([P, 4], BF16, "b_sb")
-        win_sb = sb([P, 2, 4], BF16, "win_sb")
-        nc.sync.dma_start(out=t_sb[:], in_=t.rearrange("(g p j) -> p g j", g=2, j=4))
-        nc.scalar.dma_start(out=om_sb[:], in_=om.rearrange("(p j) -> p j", j=4))
-        nc.scalar.dma_start(out=b_sb[:], in_=b.rearrange("(p j) -> p j", j=4))
-        nc.scalar.dma_start(out=win_sb[:], in_=win.rearrange("(g p j) -> p g j", g=2, j=4))
+        t_sb = sb([P, GROUPS, PACK], BF16, "t_sb")
+        om_sb = sb([P, PACK], BF16, "om_sb")
+        b_sb = sb([P, PACK], BF16, "b_sb")
+        win_sb = sb([P, GROUPS, PACK], BF16, "win_sb")
+        nc.sync.dma_start(out=t_sb[:], in_=t.rearrange("(g p j) -> p g j", g=GROUPS, j=PACK))
+        nc.scalar.dma_start(out=om_sb[:], in_=om.rearrange("(p j) -> p j", j=PACK))
+        nc.scalar.dma_start(out=b_sb[:], in_=b.rearrange("(p j) -> p j", j=PACK))
+        nc.scalar.dma_start(out=win_sb[:], in_=win.rearrange("(g p j) -> p g j", g=GROUPS, j=PACK))
 
         raw = {}
         x_raw = {}
 
-        def load_rows(key, rows):
-            raw[key] = sb([P, 4, W], BF16, "raw_%s%d%d" % key)
-            nc.sync.dma_start(out=raw[key][:], in_=rows.rearrange("(p j) d -> p j d", j=4))
-
-        def load_wg_half(a):
-            if ("w", 1, 1) not in raw:
-                raw["w", 1, 1] = [None, None]
-            raw["w", 1, 1][a] = sb([P, 4, 256], BF16, "raw_w_first%d" % a)
-            nc.sync.dma_start(out=raw["w", 1, 1][a][:],
-                              in_=wg[W:, W + a * 256:W + (a + 1) * 256].rearrange("(p j) d -> p j d", j=4))
-
-        def load_c(h):
-            load_rows(("c", 0, h), c[:, h * W:(h + 1) * W])
-
-        def load_wg(g, h):
-            load_rows(("w", g, h), wg[g * W:(g + 1) * W, h * W:(h + 1) * W])
+        def load_rows(name, source, g, h, a, parts):
+            d0 = h * HALF + a * PART
+            tile = sb([P, PACK, parts * PART], BF16, "raw_%s%d%d%d" % (name, g, h, a))
+            rows = source[g * K_PASS:(g + 1) * K_PASS, d0:d0 + parts * PART]
+            nc.sync.dma_start(out=tile[:], in_=rows.rearrange("(p j) d -> p j d", j=PACK))
+            for n in range(parts):
+                raw[name, g, h, a + n] = tile[:, :, n * PART:(n + 1) * PART]
 
         def load_x(pair):
             x_raw[pair] = sb([P, 2 * L], BF16, "x_raw%d" % pair)
             nc.sync.dma_start(out=x_raw[pair][:].rearrange("p (a l) -> p a l", a=2),
-                              in_=x[pair * 256:(pair + 1) * 256, :].rearrange("(a p) l -> p a l", a=2))
+                              in_=x[pair * 2 * P:(pair + 1) * 2 * P, :].rearrange("(a p) l -> p a l", a=2))
 
-        load_wg(0, 1)
+        load_rows("w", wg, 0, 0, 0, 1)
+        load_rows("w", wg, 0, 0, 1, 1)
+        load_rows("w", wg, 1, 0, 0, 2)
         load_x(0)
         load_x(1)
-        load_c(1)
+        load_rows("c", c, 0, 0, 0, 2)
         load_x(2)
-        load_wg_half(1)
-        load_wg_half(0)
-        load_wg(0, 0)
         load_x(3)
-        load_c(0)
-        load_wg(1, 0)
+        load_rows("w", wg, 0, 1, 0, 2)
+        load_rows("c", c, 0, 1, 0, 2)
+        load_rows("w", wg, 1, 1, 0, 2)
 
         ident_bf = sb([P, P], BF16, "ident_bf")
         ident_f = sb([P, P], F32, "ident_f")
         make_identity(nc, ident_bf[:])
         make_identity(nc, ident_f[:])
 
-        warm = sb([P, 1], F32, "warm")
-        nc.vector.memset(warm[:], 0.0)
-        nc.scalar.activation(out=warm[:], in_=warm[:], func=ACT.Sin)
+        table_load = sb([P, 1], F32, "table_load")
+        nc.vector.memset(table_load[:], 0.0)
+        nc.scalar.activation(out=table_load[:], in_=table_load[:], func=ACT.Sin)
 
-        om_decay = sb([P, 4], F32, "om_decay")
-        om_neg = sb([P, 4], F32, "om_neg")
-        win_scaled = sb([P, 2, 4], F32, "win_scaled")
-        nc.gpsimd.tensor_scalar(out=om_neg[:], in0=om_sb[:], scalar1=-1.0, scalar2=0.0, op0=ALU.mult, op1=ALU.add)
-        nc.gpsimd.tensor_scalar(out=om_decay[:], in0=om_sb[:], scalar1=-0.1, scalar2=0.0, op0=ALU.mult, op1=ALU.add)
-        nc.gpsimd.tensor_scalar(out=win_scaled[:], in0=win_sb[:], scalar1=1.0 / 32.0, scalar2=0.0, op0=ALU.mult,
-                                op1=ALU.add)
+        om_neg = sb([P, PACK], F32, "om_neg")
+        om_decay = sb([P, PACK], F32, "om_decay")
+        win_scaled = sb([P, GROUPS, PACK], F32, "win_scaled")
+        times(om_neg[:], om_sb[:], -1.0)
+        times(om_decay[:], om_sb[:], -0.1)
+        times(win_scaled[:], win_sb[:], 1.0 / 32.0)
 
-        t_all = [bank(g, [P, W], BF16, "t_all%d" % g) for g in range(2)]
-        for g in range(2):
-            for j in range(4):
+        t_all = [take_bank(("t", g, 0), [P, K_PASS], BF16) for g in range(GROUPS)]
+        for g in range(GROUPS):
+            for j in range(PACK):
                 nc.tensor.transpose(t_all[g][:, j * P:(j + 1) * P],
                                     t_sb[:, g, j:j + 1].to_broadcast([P, P]), ident_bf[:])
 
-        wave = sb([P, 4, L], F32, "wave")
-        decay = {}
+        wave = sb([P, PACK, L], F32, "wave")
+        decay = [[sb([P, PACK, PART], F32, "decay%d%d" % (g, a)) for a in range(2)] for g in range(GROUPS)]
 
-        grouped = {}
-        q_ops = {}
         e_op = operand("e", L)
-        x_op = operand("x", 8 * 256)
-        o_scales = [sb([P, R], U8, "o_scales%d" % h) for h in range(2)]
-        o_codes = {}
-        gate = {}
-        pair_tile = {}
-        res = {}
-        banks = {}
+        c_op = operand("c", D)
+        x_op = operand("x", ROW_TILES * GROUPS * P)
+        w_op = [operand("w%d" % h, GROUPS * HALF) for h in range(2)]
+        kw_op = [operand("kw%d" % h, GROUPS * HALF) for h in range(2)]
+        out_op = [operand("out%d" % h, R) for h in range(2)]
+        grouped = {}
+        results = {}
         rounded = {}
 
-        def cos_step(g, j):
-            nc.scalar.activation(out=wave[:, j, g * W:(g + 1) * W], in_=t_all[g][:], func=ACT.Sin,
+        def grouped_tile(name, index, columns):
+            if (name, index) not in grouped:
+                grouped[name, index] = sb([P, columns, PACK], BF16, "grouped_%s%d" % (name, index),
+                                          tag="grouped%d" % columns, bufs=5)
+            return grouped[name, index]
+
+        def flat(tile):
+            return tile.rearrange("p c j -> p (c j)")
+
+        rows_first = "p j (c i) -> p c j i"
+        rows_last = "p (c i) j -> p c j i"
+
+        def cos(g, j):
+            nc.scalar.activation(out=wave[:, j, g * K_PASS:(g + 1) * K_PASS], in_=t_all[g][:], func=ACT.Sin,
                                  scale=om_neg[:, j:j + 1], bias=math.pi / 2)
 
-        def amp_step(j):
+        def amplitude(j):
             nc.vector.tensor_scalar(out=wave[:, j, :], in0=wave[:, j, :], scalar1=b_sb[:, j:j + 1], scalar2=None,
                                     op0=ALU.mult)
 
-        def exp_step(g, a, n, j):
-            if (g, a) not in decay:
-                decay[g, a] = sb([P, 4, n * 256], F32, "decay%d%d" % (g, a))
-            nc.scalar.activation(out=decay[g, a][:, j, :], in_=t_all[g][:, a * 256:(a + n) * 256], func=ACT.Exp,
+        def exp(g, a, j):
+            nc.scalar.activation(out=decay[g][a][:, j, :], in_=t_all[g][:, a * PART:(a + 1) * PART], func=ACT.Exp,
                                  scale=om_decay[:, j:j + 1])
+            if a == 1 and j == PACK - 1:
+                last_read(("t", g, 0))
 
-        def e_mult(g, a):
-            if ("e", g) not in grouped:
-                grouped["e", g] = sb([P, W, 4], BF16, "e_grouped%d" % g, tag="grouped", bufs=7)
-            src = "p j (c i) -> p c j i"
-            c0 = a * 256
-            part = decay[g, a][:] if (g, a) in decay and g == 1 else decay[g, 0][:, :, c0:c0 + 256]
-            nc.vector.tensor_tensor(out=grouped["e", g][:, c0:c0 + 256, :].rearrange("p (c i) j -> p c j i", i=4),
-                                    in0=part.rearrange(src, i=4),
-                                    in1=wave[:, :, g * W + c0:g * W + c0 + 256].rearrange(src, i=4), op=ALU.mult)
+        def e_product(g, a):
+            l0 = g * K_PASS + a * PART
+            nc.vector.tensor_tensor(
+                out=grouped_tile("e", g, K_PASS)[:, a * PART:(a + 1) * PART, :].rearrange(rows_last, i=4),
+                in0=decay[g][a][:].rearrange(rows_first, i=4),
+                in1=wave[:, :, l0:l0 + PART].rearrange(rows_first, i=4), op=ALU.mult)
 
         def e_quant(g):
-            quantize(*cols(e_op, g * W, W), grouped["e", g][:].rearrange("p c j -> p (c j)"))
+            quantize(columns_of(e_op, g * K_PASS, K_PASS), flat(grouped["e", g][:]))
 
-        def interleave(key, a, engine):
-            if key not in grouped:
-                grouped[key] = sb([P, W, 4], BF16, "grouped_%s%d%d" % key, tag="grouped", bufs=7)
-            src = raw[key][a][:] if key == ("w", 1, 1) else raw[key][:, :, a * 256:(a + 1) * 256]
-            copy(engine, grouped[key][:, a * 256:(a + 1) * 256, :].rearrange("p (c i) j -> p c j i", i=4),
-                 src.rearrange("p j (c i) -> p c j i", i=4))
+        def c_group(h, engine, a):
+            out = grouped_tile("c", h, HALF)[:, a * PART:(a + 1) * PART, :]
+            copy(engine, out.rearrange(rows_last, i=4), raw["c", 0, h, a].rearrange(rows_first, i=4))
 
-        def quant(key):
-            q_ops[key] = operand("%s%d%d" % key, W)
-            quantize(q_ops[key][0][:], q_ops[key][1][:], grouped[key][:].rearrange("p c j -> p (c j)"))
+        def c_quant(h):
+            quantize(columns_of(c_op, h * HALF, HALF), flat(grouped["c", h][:]))
 
-        def x_turn(i, k):
-            banks["x", i] = bank(k, [P, 2, 2, P], F32, "x_turned%d" % i)
+        def w_group(h, engine, g, a):
+            d0 = g * HALF + a * PART
+            out = grouped_tile("w", h, GROUPS * HALF)[:, d0:d0 + PART, :]
+            copy(engine, out.rearrange(rows_last, i=4), raw["w", g, h, a].rearrange(rows_first, i=4))
+
+        def w_quant(h):
+            quantize(columns_of(w_op[h], 0, GROUPS * HALF), flat(grouped["w", h][:]))
+
+        def x_turn(i):
+            bank = take_bank(("x", i, 0), [P, GROUPS, 2, P], F32)
             words = x_raw[i // 2][:].bitcast(F32)
-            for g in range(2):
+            for g in range(GROUPS):
+                w0 = (i % 2) * (L // 2) + g * (K_PASS // 2)
                 for u in range(2):
-                    w0 = (i % 2) * W + g * 256
-                    nc.tensor.transpose(banks["x", i][:, g, u, :], words[:, w0 + u:w0 + 256:2], ident_f[:])
+                    nc.tensor.transpose(bank[:, g, u, :], words[:, w0 + u:w0 + K_PASS // 2:2], ident_f[:])
 
-        def x_copy(i, engine):
-            grouped["x", i] = sb([P, L], BF16, "x_grouped%d" % i, tag="x_grouped", bufs=9)
-            copy(engine, grouped["x", i][:].bitcast(F32).rearrange("p (g r u) -> p g r u", g=2, u=2),
-                 banks["x", i][:].rearrange("p g u r -> p g r u"))
+        def x_copy(engine, i):
+            out = grouped_tile("x", i // 2, 2 * GROUPS * P)[:, (i % 2) * GROUPS * P:(i % 2 + 1) * GROUPS * P, :]
+            copy(engine, flat(out).bitcast(F32).rearrange("p (g r u) -> p g r u", g=GROUPS, u=2),
+                 last_read(("x", i, 0))[:].rearrange("p g u r -> p g r u"))
 
-        def x_quant(i):
-            quantize(*cols(x_op, i * 256, 256), grouped["x", i][:])
+        def x_quant(pair):
+            quantize(columns_of(x_op, pair * 2 * GROUPS * P, 2 * GROUPS * P), flat(grouped["x", pair][:]))
 
-        def ker_mm(g, h, s, k):
-            banks["k", g, h, s] = bank(k, [P, 4, P], F32, "ker%d%d%d" % (g, h, s))
-            for j in range(4):
-                mm(banks["k", g, h, s][:, j, :], cols(e_op, g * W + j * P, P), cols(q_ops["c", 0, h], s * P, P), True, True)
+        def ker(h, g, s):
+            bank = take_bank(("ker", g, h * PACK + s), [P, PACK, P], F32)
+            for j in range(PACK):
+                matmul(bank[:, j, :], columns_of(e_op, g * K_PASS + j * P, P),
+                       columns_of(c_op, h * HALF + s * P, P), True, True)
 
-        def kw_mult(g, h, s):
-            if ("k", g, h) not in grouped:
-                grouped["k", g, h] = sb([P, W, 4], BF16, "grouped_k%d%d" % (g, h), tag="grouped", bufs=7)
-            nc.vector.tensor_tensor(out=grouped["k", g, h][:, s * P:(s + 1) * P, :],
-                                    in0=banks["k", g, h, s][:].rearrange("p j d -> p d j"),
-                                    in1=win_scaled[:, g, :].unsqueeze(1).to_broadcast([P, P, 4]), op=ALU.mult)
+        def kw_product(h, g, s):
+            d0 = g * HALF + s * P
+            nc.vector.tensor_tensor(out=grouped_tile("kw", h, GROUPS * HALF)[:, d0:d0 + P, :],
+                                    in0=last_read(("ker", g, h * PACK + s))[:].rearrange("p j d -> p d j"),
+                                    in1=win_scaled[:, g, :].unsqueeze(1).to_broadcast([P, P, PACK]), op=ALU.mult)
 
-        def x_product(kind, i, h, k):
-            banks[kind, i, h] = bank(k, [P, W], F32, "acc_%s%d%d" % (kind, i, h))
-            for g in range(2):
-                mm(banks[kind, i, h][:], cols(x_op, i * 256 + g * P, P), cols(q_ops[kind, g, h], 0, W), g == 0, g == 1)
+        def kw_quant(h):
+            quantize(columns_of(kw_op[h], 0, GROUPS * HALF), flat(grouped["kw", h][:]))
 
-        def gate_step(i, h):
-            if (i // 2, h) not in pair_tile:
-                pair_tile[i // 2, h] = sb([P, 2, W], F32, "gate%d%d" % (i // 2, h))
-            gate[i, h] = pair_tile[i // 2, h][:, i % 2, :]
-            nc.scalar.activation(out=gate[i, h], in_=banks["w", i, h][:], func=ACT.Tanh, scale=0.5)
+        def x_times(name, moving, i, h):
+            bank = take_bank((name, i, h), [P, HALF], F32)
+            for g in range(GROUPS):
+                matmul(bank[:], columns_of(x_op, (i * GROUPS + g) * P, P), columns_of(moving, g * HALF, HALF),
+                       g == 0, g == GROUPS - 1)
 
-        def result(i, h):
-            res[i, h] = gate[i, h]
-            nc.vector.scalar_tensor_tensor(out=res[i, h], in0=gate[i, h], scalar=1.0,
-                                           in1=banks["k", i, h][:], op0=ALU.add, op1=ALU.mult)
+        def x_wg(h, i):
+            x_times("gate", w_op[h], i, h)
 
-        def store_result(pair, h):
-            rows = out_0[pair * 256:(pair + 1) * 256, h * W:(h + 1) * W]
-            nc.sync.dma_start(out=rows.rearrange("(a p) d -> p a d", a=2), in_=pair_tile[pair, h][:])
+        def x_kw(h, i):
+            x_times("u", kw_op[h], i, h)
 
-        def round_step(i, h, engine):
-            rounded[i, h] = sb([P, W], BF16, "rounded%d%d" % (i, h), tag="rounded", bufs=16)
+        def result_of(i, h):
+            if (i // 2, h) not in results:
+                results[i // 2, h] = sb([P, 2, HALF], F32, "results%d%d" % (i // 2, h))
+            return results[i // 2, h][:, i % 2, :]
+
+        def tanh(h, i):
+            nc.scalar.activation(out=result_of(i, h), in_=last_read(("gate", i, h))[:], func=ACT.Tanh, scale=0.5)
+
+        def result(h, i):
+            nc.vector.scalar_tensor_tensor(out=result_of(i, h), in0=result_of(i, h), scalar=1.0,
+                                           in1=last_read(("u", i, h))[:], op0=ALU.add, op1=ALU.mult)
+
+        def store_result(h, pair):
+            rows = out_0[pair * 2 * P:(pair + 1) * 2 * P, h * HALF:(h + 1) * HALF]
+            nc.sync.dma_start(out=rows.rearrange("(a p) d -> p a d", a=2), in_=results[pair, h][:])
+
+        def round_result(h, engine, i):
+            rounded[i, h] = sb([P, HALF], BF16, "rounded%d%d" % (i, h))
             copy(engine, rounded[i, h][:].rearrange("r (u p e) -> r u p e", u=2, e=2),
-                 res[i, h].rearrange("r (p u e) -> r u p e", u=2, e=2))
+                 result_of(i, h).rearrange("r (p u e) -> r u p e", u=2, e=2))
 
-        def o_turn(i, n, h, k):
-            banks["o", i, h] = bank(k, [P, n, 2, P], F32, "o_turned%d%d" % (i, h))
-            for a in range(n):
+        def out_turn(h, i, tiles):
+            bank = take_bank(("out", i, h), [P, tiles, 2, P], F32)
+            for a in range(tiles):
                 words = rounded[i + a, h][:].bitcast(F32)
                 for u in range(2):
-                    nc.tensor.transpose(banks["o", i, h][:, a, u, :], words[:, u * P:(u + 1) * P], ident_f[:])
+                    nc.tensor.transpose(bank[:, a, u, :], words[:, u * P:(u + 1) * P], ident_f[:])
 
-        def o_copy(i, n, h, engine):
-            grouped["o", i, h] = sb([P, n * W], BF16, "o_grouped%d%d" % (i, h), tag="x_grouped", bufs=9)
-            copy(engine, grouped["o", i, h][:].bitcast(F32).rearrange("p (a r u) -> p a r u", a=n, u=2),
-                 banks["o", i, h][:].rearrange("p a u r -> p a r u"))
+        def out_copy(h, engine, i, tiles):
+            out = grouped_tile("out", h, R)[:, i * P:(i + tiles) * P, :]
+            copy(engine, flat(out).bitcast(F32).rearrange("p (a r u) -> p a r u", a=tiles, u=2),
+                 last_read(("out", i, h))[:].rearrange("p a u r -> p a r u"))
 
-        def o_quant(i, n, h):
-            o_codes[i, h] = sb([P, n * P], U32, "o_codes%d%d" % (i, h))
-            quantize(o_codes[i, h][:], o_scales[h][:, i * P:(i + n) * P], grouped["o", i, h][:])
+        def out_quant(h, i, tiles):
+            quantize(columns_of(out_op[h], i * P, tiles * P), flat(grouped["out", h][:, i * P:(i + tiles) * P, :]))
 
-        def store_codes(i, n, h):
-            words_out = out_1[h].rearrange("p m t -> p (m t)").bitcast(I32)
-            nc.sync.dma_start(out=words_out[:, i * P:(i + n) * P], in_=o_codes[i, h][:].bitcast(I32))
+        def store_codes(h, i, tiles):
+            words = out_1[h].rearrange("p m t -> p (m t)").bitcast(I32)
+            nc.sync.dma_start(out=words[:, i * P:(i + tiles) * P],
+                              in_=out_op[h][0][:, i * P:(i + tiles) * P].bitcast(I32))
 
-        def store_scales(h, q, engine):
-            queue = nc.sync if engine == "sp" else nc.scalar
-            queue.dma_start(out=out_2[h, 4 * q:4 * q + 4, :].bitcast(I32),
-                            in_=o_scales[h][32 * q:32 * q + 4, :].bitcast(I32))
+        def store_scales(h, engine, quadrant):
+            queue = nc.sync if engine == "y" else nc.scalar
+            queue.dma_start(out=out_2[h, 4 * quadrant:4 * quadrant + 4, :].bitcast(I32),
+                            in_=out_op[h][1][32 * quadrant:32 * quadrant + 4, :].bitcast(I32))
 
-        cos_step(0, 3)
-        interleave(("w", 0, 1), 0, "v")
-        cos_step(1, 3)
-        interleave(("w", 0, 1), 1, "v")
-        amp_step(3)
-        cos_step(1, 0)
-        quant(("w", 0, 1))
-        cos_step(0, 0)
-        amp_step(0)
-        cos_step(1, 1)
-        x_turn(1, 2)
-        x_copy(1, "v")
-        x_turn(0, 3)
-        cos_step(0, 1)
-        amp_step(1)
-        cos_step(0, 2)
-        cos_step(1, 2)
-        exp_step(0, 0, 2, 2)
-        exp_step(0, 0, 2, 3)
-        exp_step(1, 0, 1, 0)
-        x_turn(3, 4)
-        x_turn(5, 5)
-        exp_step(0, 0, 2, 0)
-        x_turn(4, 6)
-        x_quant(1)
-        amp_step(2)
-        exp_step(0, 0, 2, 1)
-        interleave(("c", 0, 1), 1, "v")
-        interleave(("w", 1, 1), 1, "v")
-        x_copy(0, "s")
-        x_copy(3, "s")
-        interleave(("c", 0, 1), 0, "v")
-        interleave(("w", 1, 1), 0, "v")
-        quant(("c", 0, 1))
-        quant(("w", 1, 1))
-        exp_step(1, 1, 1, 2)
-        x_turn(6, 7)
-        x_copy(6, "s")
-        e_mult(0, 1)
-        exp_step(1, 1, 1, 3)
-        exp_step(1, 1, 1, 0)
-        x_turn(2, 2)
-        exp_step(1, 1, 1, 1)
-        x_quant(0)
-        x_copy(5, "s")
-        exp_step(1, 0, 1, 1)
-        x_turn(7, 0)
-        e_mult(0, 0)
-        x_quant(6)
-        e_quant(0)
-        x_product("w", 0, 1, 3)
-        exp_step(1, 0, 1, 3)
-        ker_mm(0, 1, 2, 4)
-        exp_step(1, 0, 1, 2)
-        ker_mm(0, 1, 0, 7)
-        ker_mm(0, 1, 3, 5)
-        e_mult(1, 1)
-        x_copy(2, "s")
-        x_copy(7, "s")
-        gate_step(0, 1)
-        e_mult(1, 0)
-        ker_mm(0, 1, 1, 1)
-        x_quant(5)
-        x_quant(2)
-        e_quant(1)
-        x_quant(3)
-        x_product("w", 5, 1, 2)
-        ker_mm(1, 1, 3, 0)
-        kw_mult(0, 1, 0)
-        kw_mult(1, 1, 3)
-        x_product("w", 1, 1, 3)
-        interleave(("c", 0, 0), 1, "s")
-        kw_mult(0, 1, 1)
-        interleave(("c", 0, 0), 0, "s")
-        x_product("w", 6, 1, 7)
-        kw_mult(0, 1, 2)
-        gate_step(5, 1)
-        ker_mm(1, 1, 1, 0)
-        ker_mm(1, 1, 2, 2)
-        gate_step(6, 1)
-        quant(("c", 0, 0))
-        x_product("w", 2, 1, 1)
-        ker_mm(1, 1, 0, 7)
-        ker_mm(1, 0, 2, 4)
-        x_copy(4, "s")
-        x_product("w", 3, 1, 6)
-        kw_mult(0, 1, 3)
-        ker_mm(0, 0, 3, 5)
-        x_quant(4)
-        x_quant(7)
-        interleave(("w", 0, 0), 1, "s")
-        kw_mult(1, 1, 2)
-        x_product("w", 7, 1, 2)
-        gate_step(1, 1)
-        gate_step(2, 1)
-        interleave(("w", 1, 0), 0, "s")
-        gate_step(7, 1)
-        ker_mm(0, 0, 1, 3)
-        kw_mult(1, 1, 0)
-        ker_mm(1, 0, 1, 1)
-        kw_mult(1, 1, 1)
-        ker_mm(0, 0, 0, 7)
-        quant(("k", 0, 1))
-        quant(("k", 1, 1))
-        x_product("w", 4, 1, 0)
-        kw_mult(0, 0, 0)
-        kw_mult(0, 0, 3)
-        x_product("k", 7, 1, 2)
-        result(7, 1)
-        interleave(("w", 1, 0), 1, "s")
-        quant(("w", 1, 0))
-        gate_step(4, 1)
-        x_product("k", 1, 1, 7)
-        x_product("k", 0, 1, 5)
-        result(0, 1)
-        x_product("k", 4, 1, 2)
-        result(1, 1)
-        round_step(7, 1, "g")
-        interleave(("w", 0, 0), 0, "s")
-        quant(("w", 0, 0))
-        gate_step(3, 1)
-        x_product("k", 2, 1, 0)
-        x_product("k", 6, 1, 5)
-        x_product("k", 5, 1, 7)
-        result(6, 1)
-        round_step(6, 1, "s")
-        result(5, 1)
-        store_result(3, 1)
-        x_product("w", 3, 0, 6)
-        x_product("w", 4, 0, 5)
-        x_product("k", 3, 1, 7)
-        result(4, 1)
-        round_step(1, 1, "g")
-        ker_mm(1, 0, 3, 2)
-        gate_step(3, 0)
-        round_step(0, 1, "g")
-        round_step(4, 1, "g")
-        gate_step(4, 0)
-        round_step(5, 1, "s")
-        result(2, 1)
-        result(3, 1)
-        x_product("w", 1, 0, 6)
-        store_result(0, 1)
-        o_turn(0, 2, 1, 0)
-        gate_step(1, 0)
-        kw_mult(1, 0, 3)
-        o_copy(0, 2, 1, "s")
-        o_turn(6, 2, 1, 5)
-        kw_mult(1, 0, 2)
-        round_step(2, 1, "g")
-        ker_mm(0, 0, 2, 7)
-        x_product("w", 0, 0, 2)
-        o_copy(6, 2, 1, "s")
-        gate_step(0, 0)
-        store_result(2, 1)
-        kw_mult(0, 0, 1)
-        kw_mult(0, 0, 2)
-        kw_mult(1, 0, 1)
-        ker_mm(1, 0, 0, 6)
-        round_step(3, 1, "g")
-        kw_mult(1, 0, 0)
-        quant(("k", 0, 0))
-        o_turn(2, 2, 1, 4)
-        o_turn(4, 2, 1, 0)
-        o_copy(2, 2, 1, "s")
-        store_result(1, 1)
-        o_copy(4, 2, 1, "s")
-        quant(("k", 1, 0))
-        o_quant(2, 2, 1)
-        o_quant(6, 2, 1)
-        x_product("w", 2, 0, 3)
-        x_product("w", 6, 0, 5)
-        o_quant(0, 2, 1)
-        x_product("w", 5, 0, 7)
-        gate_step(2, 0)
-        gate_step(6, 0)
-        gate_step(5, 0)
-        x_product("k", 2, 0, 2)
-        x_product("k", 3, 0, 1)
-        o_quant(4, 2, 1)
-        store_scales(1, 2, "s")
-        result(2, 0)
-        x_product("k", 6, 0, 6)
-        store_codes(2, 2, 1)
-        store_scales(1, 3, "s")
-        result(3, 0)
-        round_step(3, 0, "s")
-        x_product("k", 5, 0, 4)
-        store_codes(6, 2, 1)
-        result(6, 0)
-        result(5, 0)
-        store_codes(0, 2, 1)
-        x_product("k", 4, 0, 0)
-        x_product("k", 1, 0, 3)
-        store_codes(4, 2, 1)
-        round_step(2, 0, "g")
-        store_result(1, 0)
-        store_scales(1, 1, "sp")
-        result(4, 0)
-        round_step(5, 0, "s")
-        result(1, 0)
-        x_product("k", 0, 0, 5)
-        round_step(6, 0, "g")
-        o_turn(6, 1, 0, 7)
-        o_turn(2, 2, 0, 2)
-        o_copy(6, 1, 0, "s")
-        result(0, 0)
-        store_scales(1, 0, "sp")
-        round_step(1, 0, "v")
-        o_quant(6, 1, 0)
-        o_copy(2, 2, 0, "s")
-        round_step(4, 0, "v")
-        x_product("w", 7, 0, 1)
-        gate_step(7, 0)
-        o_quant(2, 2, 0)
-        round_step(0, 0, "s")
-        store_result(2, 0)
-        store_result(0, 0)
-        x_product("k", 7, 0, 6)
-        result(7, 0)
-        round_step(7, 0, "v")
-        o_turn(4, 2, 0, 4)
-        o_turn(0, 2, 0, 0)
-        o_turn(7, 1, 0, 3)
-        o_copy(4, 2, 0, "s")
-        store_codes(6, 1, 0)
-        o_quant(4, 2, 0)
-        store_codes(2, 2, 0)
-        store_result(3, 0)
-        o_copy(0, 2, 0, "s")
-        o_quant(0, 2, 0)
-        o_copy(7, 1, 0, "s")
-        o_quant(7, 1, 0)
-        store_scales(0, 1, "s")
-        store_codes(4, 2, 0)
-        store_codes(0, 2, 0)
-        store_codes(7, 1, 0)
-        store_scales(0, 2, "s")
-        store_scales(0, 3, "s")
-        store_scales(0, 0, "sp")
+        def each(count):
+            return [(n,) for n in range(count)]
+
+        quant_units = [[(0, ROW_TILES)], PLANE_UNITS[1]]
+        by_group = [(g, n) for g in range(GROUPS) for n in range(PACK)]
+        parts = [(g, a) for g in range(GROUPS) for a in range(2)]
+        ITEMS = {
+            "cos": (cos, [(g, j) for j in range(PACK) for g in range(GROUPS)]),
+            "amplitude": (amplitude, each(PACK)),
+            "exp": (exp, [(g, a, j) for g, a in parts for j in range(PACK)]),
+            "e_product": (e_product, parts),
+            "e_quant": (e_quant, each(GROUPS)),
+            "x_turn": (x_turn, each(ROW_TILES)),
+            "x_copy": (x_copy, each(ROW_TILES)),
+            "x_quant": (x_quant, each(ROW_TILES // 2)),
+        }
+        for h in range(2):
+            for name, step, items in [
+                ("c_group", c_group, each(2)), ("c_quant", c_quant, [()]),
+                ("w_group", w_group, parts), ("w_quant", w_quant, [()]),
+                ("ker", ker, by_group), ("kw_product", kw_product, by_group), ("kw_quant", kw_quant, [()]),
+                ("x_wg", x_wg, each(ROW_TILES)), ("tanh", tanh, each(ROW_TILES)),
+                ("x_kw", x_kw, each(ROW_TILES)), ("result", result, each(ROW_TILES)),
+                ("store_result", store_result, each(ROW_TILES // 2)),
+                ("round_result", round_result, each(ROW_TILES)),
+                ("out_turn", out_turn, PLANE_UNITS[h]), ("out_copy", out_copy, PLANE_UNITS[h]),
+                ("out_quant", out_quant, quant_units[h]), ("store_codes", store_codes, quant_units[h]),
+                ("store_scales", store_scales, each(4)),
+            ]:
+                ITEMS["%s.%d" % (name, h)] = (step, items)
+
+        done = {}
+        for word in ORDER.split():
+            key, engine = (word.split(":") + [None])[:2]
+            step, items = ITEMS[key]
+            lead = [int(key.split(".")[1])] if "." in key else []
+            step(*(lead + ([engine] if engine else []) + list(items[done.get(key, 0)])))
+            done[key] = done.get(key, 0) + 1
+        assert all(done[key] == len(ITEMS[key][1]) for key in ITEMS)

import math
from contextlib import ExitStack

import concourse.mybir as mybir
from concourse.masks import make_identity

R, L, N, D = 1024, 1024, 512, 1024
FLOPS = 2 * L * N * D + 2 * 2 * R * L * D

F32 = mybir.dt.float32
BF16 = mybir.dt.bfloat16
U32 = mybir.dt.uint32
I32 = mybir.dt.int32
U8 = mybir.dt.uint8
FP8X4 = mybir.dt.float8_e4m3fn_x4
ALU = mybir.AluOpType
ACT = mybir.ActivationFunctionType

P = 128
PACK = 4
K_PASS = P * PACK
GROUPS = L // K_PASS
HALF = 512
PART = 256
ROW_TILES = R // P
BANKS = 8

PAIRS = [(i, 2) for i in range(0, ROW_TILES, 2)]
PLANE_UNITS = [PAIRS, PAIRS[:-1] + [(ROW_TILES - 2, 1), (ROW_TILES - 1, 1)]]

ORDER = """
cos cos cos cos cos cos w_group.0:v w_group.0:v amplitude cos cos exp exp w_group.0:v exp exp exp
w_group.0:v exp x_turn x_turn amplitude x_turn amplitude x_turn exp w_quant.0 c_group.0:v x_turn x_turn exp
x_copy:s x_copy:s exp c_group.0:v exp exp exp amplitude exp c_quant.0 x_turn e_product exp exp exp x_copy:s
x_copy:s e_product x_quant e_quant e_product ker.0 x_wg.0 ker.0 ker.0 x_wg.0 x_copy:s x_turn kw_product.0
e_product kw_product.0 x_copy:s ker.0 e_quant kw_product.0 c_group.1:s ker.0 x_quant ker.0 x_wg.0
kw_product.0 kw_product.0 c_group.1:s x_copy:s x_wg.0 c_quant.1 ker.0 x_quant ker.0 tanh.0 tanh.0 ker.1
x_wg.0 kw_product.0 tanh.0 kw_product.0 x_copy:s kw_product.0 tanh.0 x_quant x_wg.0 tanh.0 kw_quant.0 ker.1
ker.1 ker.1 kw_product.1 kw_product.1 x_wg.0 tanh.0 x_wg.0 x_kw.0 result.0 w_group.1:s x_kw.0 x_kw.0
round_result.0:g x_kw.0 result.0 x_kw.0 x_kw.0 round_result.0:g kw_product.1 result.0 result.0 w_group.1:s
w_group.1:s x_kw.0 w_group.1:s round_result.0:g result.0 w_quant.1 tanh.0 ker.1 ker.1 ker.1 tanh.0 result.0
round_result.0:s round_result.0:s result.0 x_kw.0 x_wg.1 round_result.0:g result.0 round_result.0:g x_wg.1
tanh.1 store_result.0 x_wg.1 tanh.1 kw_product.1 kw_product.1 round_result.0:g tanh.1 ker.1 out_turn.0
store_result.0 store_result.0 store_result.0 out_copy.0:s out_turn.0 out_turn.0 out_turn.0 out_copy.0:s
out_copy.0:s x_wg.1 out_copy.0:s x_wg.1 tanh.1 kw_product.1 kw_product.1 x_wg.1 kw_product.1 kw_quant.1
x_wg.1 out_quant.0 x_kw.1 store_scales.0:y x_kw.1 x_kw.1 result.1 result.1 tanh.1 x_kw.1 tanh.1 tanh.1
store_scales.0:s store_scales.0:y round_result.1:g store_scales.0:s result.1 result.1 x_kw.1 x_kw.1
store_codes.0 round_result.1:g result.1 store_result.1 round_result.1:s result.1 out_turn.1 round_result.1:s
out_turn.1 out_copy.1:v store_result.1 out_quant.1 out_copy.1:s store_result.1 x_wg.1 out_quant.1
round_result.1:g x_kw.1 x_kw.1 store_codes.1 round_result.1:s store_codes.1 result.1 tanh.1 result.1
out_turn.1 round_result.1:v out_turn.1 store_result.1 round_result.1:v out_copy.1:s out_quant.1 out_turn.1
out_copy.1:v out_quant.1 out_copy.1:s out_quant.1 store_codes.1 store_codes.1 store_scales.1:s store_codes.1
store_scales.1:s store_scales.1:y store_scales.1:s
"""


def tile_constantqmodalstatespacegatedreadout_x1_kernel(tc, x, t, om, b, c, win, wg, out_0, out_1, out_2):
    nc = tc.nc
    with ExitStack() as ctx:
        sbuf = ctx.enter_context(tc.tile_pool(name="sbuf", bufs=1))
        psum = ctx.enter_context(tc.psum_pool(name="psum", bufs=1))
        ctx.enter_context(tc.manual_schedule())

        def sb(shape, dtype, name, tag=None, bufs=1):
            return sbuf.tile(shape, dtype, name=name, tag=tag or name, bufs=bufs, align_bytes=64)

        free_banks = list(range(BANKS))
        held = {}

        def take_bank(key, shape, dtype):
            number = free_banks[0]
            free_banks.remove(number)
            held[key] = (number, psum.tile(shape, dtype, name="psum_%s_%d_%d" % key, tag="bank%d" % number))
            return held[key][1]

        def last_read(key):
            free_banks.append(held[key][0])
            return held[key][1]

        def operand(name, columns):
            return (sb([P, columns], U32, name + "_codes"), sb([P, columns], U8, name + "_scales"))

        def columns_of(op, start, count):
            return (op[0][:, start:start + count], op[1][:, start:start + count])

        def quantize(op, grouped):
            nc.vector.quantize_mx(out=op[0].bitcast(FP8X4), scales=op[1], in_=grouped)

        def matmul(out, stationary, moving, start, stop):
            nc.tensor.matmul_mx(out=out, lhsT=stationary[0].bitcast(FP8X4), lhsT_scale=stationary[1],
                                rhs=moving[0].bitcast(FP8X4), rhs_scale=moving[1], start=start, stop=stop)

        def copy(engine, out, in_):
            if engine == "v":
                nc.vector.tensor_copy(out=out, in_=in_)
            elif engine == "s":
                nc.scalar.copy(out=out, in_=in_)
            else:
                times(out, in_, 1.0)

        def times(out, in_, factor):
            nc.gpsimd.tensor_scalar(out=out, in0=in_, scalar1=factor, scalar2=0.0, op0=ALU.mult, op1=ALU.add)

        t_sb = sb([P, GROUPS, PACK], BF16, "t_sb")
        om_sb = sb([P, PACK], BF16, "om_sb")
        b_sb = sb([P, PACK], BF16, "b_sb")
        win_sb = sb([P, GROUPS, PACK], BF16, "win_sb")
        nc.sync.dma_start(out=t_sb[:], in_=t.rearrange("(g p j) -> p g j", g=GROUPS, j=PACK))
        nc.scalar.dma_start(out=om_sb[:], in_=om.rearrange("(p j) -> p j", j=PACK))
        nc.scalar.dma_start(out=b_sb[:], in_=b.rearrange("(p j) -> p j", j=PACK))
        nc.scalar.dma_start(out=win_sb[:], in_=win.rearrange("(g p j) -> p g j", g=GROUPS, j=PACK))

        raw = {}
        x_raw = {}

        def load_rows(name, source, g, h, a, parts):
            d0 = h * HALF + a * PART
            tile = sb([P, PACK, parts * PART], BF16, "raw_%s%d%d%d" % (name, g, h, a))
            rows = source[g * K_PASS:(g + 1) * K_PASS, d0:d0 + parts * PART]
            nc.sync.dma_start(out=tile[:], in_=rows.rearrange("(p j) d -> p j d", j=PACK))
            for n in range(parts):
                raw[name, g, h, a + n] = tile[:, :, n * PART:(n + 1) * PART]

        def load_x(pair):
            x_raw[pair] = sb([P, 2 * L], BF16, "x_raw%d" % pair)
            nc.sync.dma_start(out=x_raw[pair][:].rearrange("p (a l) -> p a l", a=2),
                              in_=x[pair * 2 * P:(pair + 1) * 2 * P, :].rearrange("(a p) l -> p a l", a=2))

        load_rows("w", wg, 0, 0, 0, 1)
        load_rows("w", wg, 0, 0, 1, 1)
        load_rows("w", wg, 1, 0, 0, 2)
        load_x(0)
        load_x(1)
        load_rows("c", c, 0, 0, 0, 2)
        load_x(2)
        load_x(3)
        load_rows("w", wg, 0, 1, 0, 2)
        load_rows("c", c, 0, 1, 0, 2)
        load_rows("w", wg, 1, 1, 0, 2)

        ident_bf = sb([P, P], BF16, "ident_bf")
        ident_f = sb([P, P], F32, "ident_f")
        make_identity(nc, ident_bf[:])
        make_identity(nc, ident_f[:])

        table_load = sb([P, 1], F32, "table_load")
        nc.vector.memset(table_load[:], 0.0)
        nc.scalar.activation(out=table_load[:], in_=table_load[:], func=ACT.Sin)

        om_neg = sb([P, PACK], F32, "om_neg")
        om_decay = sb([P, PACK], F32, "om_decay")
        win_scaled = sb([P, GROUPS, PACK], F32, "win_scaled")
        times(om_neg[:], om_sb[:], -1.0)
        times(om_decay[:], om_sb[:], -0.1)
        times(win_scaled[:], win_sb[:], 1.0 / 32.0)

        t_all = [take_bank(("t", g, 0), [P, K_PASS], BF16) for g in range(GROUPS)]
        for g in range(GROUPS):
            for j in range(PACK):
                nc.tensor.transpose(t_all[g][:, j * P:(j + 1) * P],
                                    t_sb[:, g, j:j + 1].to_broadcast([P, P]), ident_bf[:])

        wave = sb([P, PACK, L], F32, "wave")
        decay = [[sb([P, PACK, PART], F32, "decay%d%d" % (g, a)) for a in range(2)] for g in range(GROUPS)]

        e_op = operand("e", L)
        c_op = operand("c", D)
        x_op = operand("x", ROW_TILES * GROUPS * P)
        w_op = [operand("w%d" % h, GROUPS * HALF) for h in range(2)]
        kw_op = [operand("kw%d" % h, GROUPS * HALF) for h in range(2)]
        out_op = [operand("out%d" % h, R) for h in range(2)]
        grouped = {}
        results = {}
        rounded = {}

        def grouped_tile(name, index, columns):
            if (name, index) not in grouped:
                grouped[name, index] = sb([P, columns, PACK], BF16, "grouped_%s%d" % (name, index),
                                          tag="grouped%d" % columns, bufs=5)
            return grouped[name, index]

        def flat(tile):
            return tile.rearrange("p c j -> p (c j)")

        rows_first = "p j (c i) -> p c j i"
        rows_last = "p (c i) j -> p c j i"

        def cos(g, j):
            nc.scalar.activation(out=wave[:, j, g * K_PASS:(g + 1) * K_PASS], in_=t_all[g][:], func=ACT.Sin,
                                 scale=om_neg[:, j:j + 1], bias=math.pi / 2)

        def amplitude(j):
            nc.vector.tensor_scalar(out=wave[:, j, :], in0=wave[:, j, :], scalar1=b_sb[:, j:j + 1], scalar2=None,
                                    op0=ALU.mult)

        def exp(g, a, j):
            nc.scalar.activation(out=decay[g][a][:, j, :], in_=t_all[g][:, a * PART:(a + 1) * PART], func=ACT.Exp,
                                 scale=om_decay[:, j:j + 1])
            if a == 1 and j == PACK - 1:
                last_read(("t", g, 0))

        def e_product(g, a):
            l0 = g * K_PASS + a * PART
            nc.vector.tensor_tensor(
                out=grouped_tile("e", g, K_PASS)[:, a * PART:(a + 1) * PART, :].rearrange(rows_last, i=4),
                in0=decay[g][a][:].rearrange(rows_first, i=4),
                in1=wave[:, :, l0:l0 + PART].rearrange(rows_first, i=4), op=ALU.mult)

        def e_quant(g):
            quantize(columns_of(e_op, g * K_PASS, K_PASS), flat(grouped["e", g][:]))

        def c_group(h, engine, a):
            out = grouped_tile("c", h, HALF)[:, a * PART:(a + 1) * PART, :]
            copy(engine, out.rearrange(rows_last, i=4), raw["c", 0, h, a].rearrange(rows_first, i=4))

        def c_quant(h):
            quantize(columns_of(c_op, h * HALF, HALF), flat(grouped["c", h][:]))

        def w_group(h, engine, g, a):
            d0 = g * HALF + a * PART
            out = grouped_tile("w", h, GROUPS * HALF)[:, d0:d0 + PART, :]
            copy(engine, out.rearrange(rows_last, i=4), raw["w", g, h, a].rearrange(rows_first, i=4))

        def w_quant(h):
            quantize(columns_of(w_op[h], 0, GROUPS * HALF), flat(grouped["w", h][:]))

        def x_turn(i):
            bank = take_bank(("x", i, 0), [P, GROUPS, 2, P], F32)
            words = x_raw[i // 2][:].bitcast(F32)
            for g in range(GROUPS):
                w0 = (i % 2) * (L // 2) + g * (K_PASS // 2)
                for u in range(2):
                    nc.tensor.transpose(bank[:, g, u, :], words[:, w0 + u:w0 + K_PASS // 2:2], ident_f[:])

        def x_copy(engine, i):
            out = grouped_tile("x", i // 2, 2 * GROUPS * P)[:, (i % 2) * GROUPS * P:(i % 2 + 1) * GROUPS * P, :]
            copy(engine, flat(out).bitcast(F32).rearrange("p (g r u) -> p g r u", g=GROUPS, u=2),
                 last_read(("x", i, 0))[:].rearrange("p g u r -> p g r u"))

        def x_quant(pair):
            quantize(columns_of(x_op, pair * 2 * GROUPS * P, 2 * GROUPS * P), flat(grouped["x", pair][:]))

        def ker(h, g, s):
            bank = take_bank(("ker", g, h * PACK + s), [P, PACK, P], F32)
            for j in range(PACK):
                matmul(bank[:, j, :], columns_of(e_op, g * K_PASS + j * P, P),
                       columns_of(c_op, h * HALF + s * P, P), True, True)

        def kw_product(h, g, s):
            d0 = g * HALF + s * P
            nc.vector.tensor_tensor(out=grouped_tile("kw", h, GROUPS * HALF)[:, d0:d0 + P, :],
                                    in0=last_read(("ker", g, h * PACK + s))[:].rearrange("p j d -> p d j"),
                                    in1=win_scaled[:, g, :].unsqueeze(1).to_broadcast([P, P, PACK]), op=ALU.mult)

        def kw_quant(h):
            quantize(columns_of(kw_op[h], 0, GROUPS * HALF), flat(grouped["kw", h][:]))

        def x_times(name, moving, i, h):
            bank = take_bank((name, i, h), [P, HALF], F32)
            for g in range(GROUPS):
                matmul(bank[:], columns_of(x_op, (i * GROUPS + g) * P, P), columns_of(moving, g * HALF, HALF),
                       g == 0, g == GROUPS - 1)

        def x_wg(h, i):
            x_times("gate", w_op[h], i, h)

        def x_kw(h, i):
            x_times("u", kw_op[h], i, h)

        def result_of(i, h):
            if (i // 2, h) not in results:
                results[i // 2, h] = sb([P, 2, HALF], F32, "results%d%d" % (i // 2, h))
            return results[i // 2, h][:, i % 2, :]

        def tanh(h, i):
            nc.scalar.activation(out=result_of(i, h), in_=last_read(("gate", i, h))[:], func=ACT.Tanh, scale=0.5)

        def result(h, i):
            nc.vector.scalar_tensor_tensor(out=result_of(i, h), in0=result_of(i, h), scalar=1.0,
                                           in1=last_read(("u", i, h))[:], op0=ALU.add, op1=ALU.mult)

        def store_result(h, pair):
            rows = out_0[pair * 2 * P:(pair + 1) * 2 * P, h * HALF:(h + 1) * HALF]
            nc.sync.dma_start(out=rows.rearrange("(a p) d -> p a d", a=2), in_=results[pair, h][:])

        def round_result(h, engine, i):
            rounded[i, h] = sb([P, HALF], BF16, "rounded%d%d" % (i, h))
            copy(engine, rounded[i, h][:].rearrange("r (u p e) -> r u p e", u=2, e=2),
                 result_of(i, h).rearrange("r (p u e) -> r u p e", u=2, e=2))

        def out_turn(h, i, tiles):
            bank = take_bank(("out", i, h), [P, tiles, 2, P], F32)
            for a in range(tiles):
                words = rounded[i + a, h][:].bitcast(F32)
                for u in range(2):
                    nc.tensor.transpose(bank[:, a, u, :], words[:, u * P:(u + 1) * P], ident_f[:])

        def out_copy(h, engine, i, tiles):
            out = grouped_tile("out", h, R)[:, i * P:(i + tiles) * P, :]
            copy(engine, flat(out).bitcast(F32).rearrange("p (a r u) -> p a r u", a=tiles, u=2),
                 last_read(("out", i, h))[:].rearrange("p a u r -> p a r u"))

        def out_quant(h, i, tiles):
            quantize(columns_of(out_op[h], i * P, tiles * P), flat(grouped["out", h][:, i * P:(i + tiles) * P, :]))

        def store_codes(h, i, tiles):
            words = out_1[h].rearrange("p m t -> p (m t)").bitcast(I32)
            nc.sync.dma_start(out=words[:, i * P:(i + tiles) * P],
                              in_=out_op[h][0][:, i * P:(i + tiles) * P].bitcast(I32))

        def store_scales(h, engine, quadrant):
            queue = nc.sync if engine == "y" else nc.scalar
            queue.dma_start(out=out_2[h, 4 * quadrant:4 * quadrant + 4, :].bitcast(I32),
                            in_=out_op[h][1][32 * quadrant:32 * quadrant + 4, :].bitcast(I32))

        def each(count):
            return [(n,) for n in range(count)]

        quant_units = [[(0, ROW_TILES)], PLANE_UNITS[1]]
        by_group = [(g, n) for g in range(GROUPS) for n in range(PACK)]
        parts = [(g, a) for g in range(GROUPS) for a in range(2)]
        ITEMS = {
            "cos": (cos, [(g, j) for j in range(PACK) for g in range(GROUPS)]),
            "amplitude": (amplitude, each(PACK)),
            "exp": (exp, [(g, a, j) for g, a in parts for j in range(PACK)]),
            "e_product": (e_product, parts),
            "e_quant": (e_quant, each(GROUPS)),
            "x_turn": (x_turn, each(ROW_TILES)),
            "x_copy": (x_copy, each(ROW_TILES)),
            "x_quant": (x_quant, each(ROW_TILES // 2)),
        }
        for h in range(2):
            for name, step, items in [
                ("c_group", c_group, each(2)), ("c_quant", c_quant, [()]),
                ("w_group", w_group, parts), ("w_quant", w_quant, [()]),
                ("ker", ker, by_group), ("kw_product", kw_product, by_group), ("kw_quant", kw_quant, [()]),
                ("x_wg", x_wg, each(ROW_TILES)), ("tanh", tanh, each(ROW_TILES)),
                ("x_kw", x_kw, each(ROW_TILES)), ("result", result, each(ROW_TILES)),
                ("store_result", store_result, each(ROW_TILES // 2)),
                ("round_result", round_result, each(ROW_TILES)),
                ("out_turn", out_turn, PLANE_UNITS[h]), ("out_copy", out_copy, PLANE_UNITS[h]),
                ("out_quant", out_quant, quant_units[h]), ("store_codes", store_codes, quant_units[h]),
                ("store_scales", store_scales, each(4)),
            ]:
                ITEMS["%s.%d" % (name, h)] = (step, items)

        done = {}
        for word in ORDER.split():
            key, engine = (word.split(":") + [None])[:2]
            step, items = ITEMS[key]
            lead = [int(key.split(".")[1])] if "." in key else []
            step(*(lead + ([engine] if engine else []) + list(items[done.get(key, 0)])))
            done[key] = done.get(key, 0) + 1
        assert all(done[key] == len(ITEMS[key][1]) for key in ITEMS)
